import numpy as np
import ml_dtypes


def mxq(x, axis, fmt="e4m3"):
    dtype, down = {"e4m3": (ml_dtypes.float8_e4m3fn, 7), "e5m2": (ml_dtypes.float8_e5m2, 14)}[fmt]
    v = np.moveaxis(np.asarray(x, np.float32).astype(ml_dtypes.bfloat16).astype(np.float64), axis, -1)
    blocks = v.reshape(v.shape[:-1] + (-1, 32))
    amax = np.abs(blocks).max(-1, keepdims=True)
    byte = np.maximum(np.where(amax > 0, np.frexp(amax)[1] - 1 + 127, 0) - down, 1)
    scale = np.exp2(byte - 127.0)
    codes = (blocks / scale).astype(np.float32).astype(dtype).astype(np.float64)
    return np.moveaxis((codes * scale).reshape(v.shape), -1, axis)


WIDE = False


def mx_kscale(k):
    if not WIDE:
        return np.ones(k)
    levels = np.array([10, -10, 5, -5, 0])
    if k % 512:
        return np.exp2(np.random.permutation(np.resize(levels, k // 32))).repeat(32)
    a = np.empty((k // 512, 16))
    for p in range(k // 512):
        a[p, :8] = np.random.permutation(np.resize(levels, 8))
        for g in range(8):
            far = levels[np.abs(levels - a[p, g]) >= 10]
            a[p, g + 8] = far[np.random.randint(len(far))]
    return np.exp2(a.ravel()).repeat(32)


def f64(x):
    return np.asarray(x).astype(np.float64)


def striped(idx):
    return np.tile(np.asarray(idx).reshape(-1, 16).T, (8, 1)).astype(np.uint16)


def unstriped(offs):
    return offs[:16].T.reshape(-1).astype(np.int64)


E2M1 = np.array([0.0, 0.5, 1.0, 1.5, 2.0, 3.0, 4.0, 6.0, -0.0, -0.5, -1.0, -1.5, -2.0, -3.0, -4.0, -6.0])


def pack_weight(w, fmt):
    k, n = w.shape
    w = f64(np.asarray(w, np.float32).astype(ml_dtypes.bfloat16)).reshape(k // 32, 32, n)
    amax = np.abs(w).max(1)
    if fmt == "e4m3":
        byte = np.frexp(amax)[1] - 1 + 127 - 7
    else:
        mant, ex = np.frexp(amax / 6.0)
        byte = np.where(mant > 0.5, ex, ex - 1) + 127
    byte = np.clip(np.where(amax > 0, byte, 1), 1, 254)
    scaled = (w * np.exp2(127.0 - byte)[:, None, :]).reshape(k, n).astype(np.float32)
    by_word = np.ascontiguousarray(scaled.reshape(k // 512, 128, 4, n).transpose(0, 1, 3, 2))
    if fmt == "e4m3":
        words = by_word.astype(ml_dtypes.float8_e4m3fn).view(np.uint8)
    else:
        c = by_word.astype(ml_dtypes.float4_e2m1fn).view(np.uint8) & 0xF
        words = (c[..., 0::2] | (c[..., 1::2] << 4)).reshape(k // 512, 128, 2 * n)
    return np.ascontiguousarray(words), np.ascontiguousarray(byte.astype(np.uint8).reshape(k // 512, 16, n))


def unpack_weight(words, scales, fmt):
    g, _, n = scales.shape
    words = np.ascontiguousarray(words).reshape(g, 128, n, -1)
    if fmt == "e4m3":
        vals = words.view(ml_dtypes.float8_e4m3fn).astype(np.float64)
    else:
        nib = np.empty((g, 128, n, 4), np.uint8)
        nib[..., 0::2] = words & 0xF
        nib[..., 1::2] = words >> 4
        vals = E2M1[nib]
    vals = vals * np.repeat(np.exp2(scales.astype(np.float64) - 127.0), 8, axis=1)[..., None]
    return vals.transpose(0, 1, 3, 2).reshape(g * 512, n)


def sigmoid(v):
    return 1.0 / (1.0 + np.exp(-v))


B, N, T, D, NQ = 1, 512, 2048, 1024, 128


def setup_inputs():
    n = np.random.standard_normal
    idx = np.random.permutation(T)[:B * N]
    s = mx_kscale(D)[:, None]
    kp = pack_weight(n((D, T)) / s, "e2m1")
    cp = pack_weight(n((D, T)) / s, "e4m3")
    return {
        "qT": (n((B, D, NQ)) * s * (1.00 / np.sqrt(D))).astype(np.float32),
        "k_words": np.ascontiguousarray(kp[0].reshape(1, 2, 128, T, 2).transpose(0, 2, 3, 1, 4)).reshape(1, 128, T, 4),
        "k_scales": kp[1],
        "c_words": cp[0],
        "c_scales": cp[1],
        "offs": striped(idx),
    }


def reference(qT, k_words, k_scales, c_words, c_scales, offs):
    idx = unstriped(offs)
    pick = lambda x, which: x[:, which].reshape(x.shape[0], B, -1).transpose(1, 0, 2)
    k = unpack_weight(k_words.reshape(1, 128, T, 2, 2).transpose(0, 3, 1, 2, 4).reshape(2, 128, 2 * T), k_scales, "e2m1")
    kg = pick(k, idx)
    c = unpack_weight(c_words, c_scales, "e4m3")
    cg = pick(c, idx)
    qq = mxq(f64(qT), 1, "e4m3")
    a = qq.transpose(0, 2, 1) @ kg
    z = qq.transpose(0, 2, 1) @ cg
    y = sigmoid(a) * z
    return y

@@ -1,0 +1,126 @@
+from contextlib import ExitStack
+
+import concourse.mybir as mybir
+
+NQ, D, T, N = 128, 1024, 2048, 512
+FLOPS = 2 * 2 * NQ * D * N
+
+F32 = mybir.dt.float32
+BF16 = mybir.dt.bfloat16
+I32 = mybir.dt.int32
+U32 = mybir.dt.uint32
+U16 = mybir.dt.uint16
+U8 = mybir.dt.uint8
+FP8X4 = mybir.dt.float8_e4m3fn_x4
+FP4X4 = mybir.dt.float4_e2m1fn_x4
+ACT = mybir.ActivationFunctionType
+MULT = mybir.AluOpType.mult
+
+P = 128
+PACK = 4
+PASSES = D // (P * PACK)
+HALF = N // 2
+C_ROW = 8
+
+
+def tile_attend_neu_mix_topk_kernel(tc, qT, k_words, k_scales, c_words, c_scales, offs, out):
+    nc = tc.nc
+    with ExitStack() as ctx:
+        sb = ctx.enter_context(tc.tile_pool(name="sb", bufs=1))
+        ps = ctx.enter_context(tc.psum_pool(name="ps", bufs=1))
+
+        offsets = sb.tile([P, N // 16], U16, name="offsets")
+        nc.sync.dma_start(offsets[:], offs)
+
+        ks = sb.tile([P, PASSES, T // 4], I32, name="ks", align_bytes=64)
+        cs = sb.tile([P, T // 4], I32, name="cs", align_bytes=64)
+        warm = sb.tile([P, 8], F32, name="warm")
+        warm_out = sb.tile([P, 8], F32, name="warm_out")
+        nc.vector.memset(ks[:], 0)
+        nc.vector.memset(cs[:], 0)
+        nc.vector.memset(warm[:], 0.0)
+        for quad in range(4):
+            rows = slice(4 * quad, 4 * quad + 4)
+            nc.scalar.dma_start(
+                ks[32 * quad : 32 * quad + 4, :, :],
+                k_scales[:, rows, :].rearrange("o f t -> f o t").bitcast(I32),
+            )
+        for quad in range(4):
+            rows = slice(4 * quad, 4 * quad + 4)
+            first = 32 * quad + C_ROW
+            nc.gpsimd.dma_start(cs[first : first + 8, :], c_scales[:, rows, :].bitcast(I32))
+        nc.scalar.activation(warm_out[:], warm[:], ACT.Sigmoid)
+
+        kw = sb.tile([P, T], I32, name="kw", align_bytes=64)
+        nc.sync.dma_start(kw[:], k_words[0].rearrange("p t b -> p (t b)").bitcast(I32))
+        q_raw = sb.tile([P, PASSES, PACK, NQ], F32, name="q_raw", align_bytes=64)
+        nc.sync.dma_start(q_raw[:], qT[0].rearrange("(o p j) w -> p o j w", o=PASSES, j=PACK))
+        cw = []
+        for o in range(PASSES):
+            words = sb.tile([P, T], I32, name=f"cw{o}", align_bytes=64)
+            nc.sync.dma_start(words[:], c_words[o].rearrange("p t b -> p (t b)").bitcast(I32))
+            cw.append(words)
+
+        ksg = sb.tile([P, PASSES, N], U8, name="ksg", align_bytes=64)
+        for o in range(PASSES):
+            nc.vector.tensor_copy(ksg[:, o, :], ks[:, o, :].bitcast(U8).indirect(offsets[:]))
+        kwg = sb.tile([P, N], U32, name="kwg", align_bytes=64)
+        nc.vector.tensor_copy(kwg[:], kw[:].bitcast(U32).indirect(offsets[:]))
+        k_codes = sb.tile([P, PASSES, N], U16, name="k_codes", align_bytes=64)
+        nc.vector.tensor_copy(k_codes[:], kwg[:].bitcast(U16).rearrange("p (n o) -> p o n", o=PASSES))
+
+        q_bf = sb.tile([P, PASSES, NQ, PACK], BF16, name="q_bf", align_bytes=64)
+        for o in range(PASSES):
+            nc.scalar.activation(q_bf[:, o, :, :], q_raw[:, o, :, :].rearrange("p j w -> p w j"), ACT.Copy)
+        q_codes = sb.tile([P, PASSES * NQ], U32, name="q_codes", align_bytes=64)
+        q_scales = sb.tile([P, PASSES * NQ], U8, name="q_scales", align_bytes=64)
+        nc.vector.quantize_mx(
+            out=q_codes[:].bitcast(FP8X4),
+            scales=q_scales[:],
+            in_=q_bf[:].rearrange("p o w j -> p (o w j)"),
+        )
+
+        a_ps = ps.tile([P, N], F32, name="a_ps")
+        for o in range(PASSES):
+            cols = slice(o * NQ, (o + 1) * NQ)
+            nc.tensor.matmul_mx(
+                out=a_ps[:],
+                lhsT=q_codes[:, cols].bitcast(FP8X4),
+                lhsT_scale=q_scales[:, cols],
+                rhs=k_codes[:, o, :].bitcast(FP4X4),
+                rhs_scale=ksg[:, o, :],
+                start=(o == 0),
+                stop=(o == PASSES - 1),
+            )
+        gate = sb.tile([P, N], F32, name="gate")
+        nc.scalar.activation(gate[:], a_ps[:], ACT.Sigmoid)
+
+        z_ps = [ps.tile([P, N], F32, name=f"z_ps{h}") for h in range(2)]
+        cwg = [sb.tile([P, N], U32, name=f"cwg{o}", align_bytes=64) for o in range(PASSES)]
+        nc.vector.tensor_copy(cwg[0][:], cw[0][:].bitcast(U32).indirect(offsets[:]))
+        csg = sb.tile([P, N], U8, name="csg", align_bytes=64)
+        nc.vector.tensor_copy(csg[:], cs[:].bitcast(U8).indirect(offsets[:]))
+        for h in range(2):
+            slots = slice(h * HALF, (h + 1) * HALF)
+            nc.vector.tensor_copy(
+                cwg[1][:, slots],
+                cw[1][:].bitcast(U32).indirect(offsets[:, h * HALF // 16 : (h + 1) * HALF // 16]),
+            )
+        for o in range(PASSES):
+            cols = slice(o * NQ, (o + 1) * NQ)
+            for h in range(2):
+                slots = slice(h * HALF, (h + 1) * HALF)
+                nc.tensor.matmul_mx(
+                    out=z_ps[h][:, :HALF],
+                    lhsT=q_codes[:, cols].bitcast(FP8X4),
+                    lhsT_scale=q_scales[:, cols],
+                    rhs=cwg[o][:, slots].bitcast(FP8X4),
+                    rhs_scale=csg[C_ROW + 4 * o :, slots],
+                    start=(o == 0),
+                    stop=(o == PASSES - 1),
+                )
+        res = sb.tile([P, N], F32, name="res")
+        for h in range(2):
+            slots = slice(h * HALF, (h + 1) * HALF)
+            nc.vector.tensor_tensor(res[:, slots], z_ps[h][:, :HALF], gate[:, slots], MULT)
+            nc.sync.dma_start(out[0][:, slots], res[:, slots])

@@ -32,6 +32,8 @@ def tile_attend_neu_mix_topk_kernel(tc, qT, k_words, k_scales, c_words, c_scales
         offsets = sb.tile([P, N // 16], U16, name="offsets")
         nc.sync.dma_start(offsets[:], offs)
 
+        kw = sb.tile([P, T], I32, name="kw", align_bytes=64)
+        nc.sync.dma_start(kw[:], k_words[0].rearrange("p t b -> p (t b)").bitcast(I32))
         ks = sb.tile([P, PASSES, T // 4], I32, name="ks", align_bytes=64)
         cs = sb.tile([P, T // 4], I32, name="cs", align_bytes=64)
         warm = sb.tile([P, 8], F32, name="warm")
@@ -41,33 +43,29 @@ def tile_attend_neu_mix_topk_kernel(tc, qT, k_words, k_scales, c_words, c_scales
         nc.vector.memset(warm[:], 0.0)
         for quad in range(4):
             rows = slice(4 * quad, 4 * quad + 4)
-            nc.scalar.dma_start(
+            nc.sync.dma_start(
                 ks[32 * quad : 32 * quad + 4, :, :],
                 k_scales[:, rows, :].rearrange("o f t -> f o t").bitcast(I32),
             )
+        nc.scalar.activation(warm_out[:], warm[:], ACT.Sigmoid)
+
+        q_raw = sb.tile([P, PASSES, PACK, NQ], F32, name="q_raw", align_bytes=64)
+        nc.sync.dma_start(q_raw[:], qT[0].rearrange("(o p j) w -> p o j w", o=PASSES, j=PACK))
+        cw = [sb.tile([P, T], I32, name=f"cw{o}", align_bytes=64) for o in range(PASSES)]
+        nc.sync.dma_start(cw[0][:], c_words[0].rearrange("p t b -> p (t b)").bitcast(I32))
         for quad in range(4):
             rows = slice(4 * quad, 4 * quad + 4)
             first = 32 * quad + C_ROW
-            nc.gpsimd.dma_start(cs[first : first + 8, :], c_scales[:, rows, :].bitcast(I32))
-        nc.scalar.activation(warm_out[:], warm[:], ACT.Sigmoid)
-
-        kw = sb.tile([P, T], I32, name="kw", align_bytes=64)
-        nc.sync.dma_start(kw[:], k_words[0].rearrange("p t b -> p (t b)").bitcast(I32))
-        q_raw = sb.tile([P, PASSES, PACK, NQ], F32, name="q_raw", align_bytes=64)
-        nc.sync.dma_start(q_raw[:], qT[0].rearrange("(o p j) w -> p o j w", o=PASSES, j=PACK))
-        cw = []
-        for o in range(PASSES):
-            words = sb.tile([P, T], I32, name=f"cw{o}", align_bytes=64)
-            nc.sync.dma_start(words[:], c_words[o].rearrange("p t b -> p (t b)").bitcast(I32))
-            cw.append(words)
+            nc.sync.dma_start(cs[first : first + 8, :], c_scales[:, rows, :].bitcast(I32))
+        nc.sync.dma_start(cw[1][:], c_words[1].rearrange("p t b -> p (t b)").bitcast(I32))
 
         ksg = sb.tile([P, PASSES, N], U8, name="ksg", align_bytes=64)
-        for o in range(PASSES):
-            nc.vector.tensor_copy(ksg[:, o, :], ks[:, o, :].bitcast(U8).indirect(offsets[:]))
         kwg = sb.tile([P, N], U32, name="kwg", align_bytes=64)
-        nc.vector.tensor_copy(kwg[:], kw[:].bitcast(U32).indirect(offsets[:]))
         k_codes = sb.tile([P, PASSES, N], U16, name="k_codes", align_bytes=64)
+        nc.vector.tensor_copy(kwg[:], kw[:].bitcast(U32).indirect(offsets[:]))
+        nc.vector.tensor_copy(ksg[:, 0, :], ks[:, 0, :].bitcast(U8).indirect(offsets[:]))
         nc.vector.tensor_copy(k_codes[:], kwg[:].bitcast(U16).rearrange("p (n o) -> p o n", o=PASSES))
+        nc.vector.tensor_copy(ksg[:, 1, :], ks[:, 1, :].bitcast(U8).indirect(offsets[:]))
 
         q_bf = sb.tile([P, PASSES, NQ, PACK], BF16, name="q_bf", align_bytes=64)
         for o in range(PASSES):

@@ -30,10 +30,12 @@ def tile_attend_neu_mix_topk_kernel(tc, qT, k_words, k_scales, c_words, c_scales
         ps = ctx.enter_context(tc.psum_pool(name="ps", bufs=1))
 
         offsets = sb.tile([P, N // 16], U16, name="offsets")
-        nc.sync.dma_start(offsets[:], offs)
 
-        kw = sb.tile([P, T], I32, name="kw", align_bytes=64)
-        nc.sync.dma_start(kw[:], k_words[0].rearrange("p t b -> p (t b)").bitcast(I32))
+        q_hbm = qT[0].rearrange("(o p j) w -> o p j w", o=PASSES, j=PACK)
+        q_raw = [sb.tile([P, PACK, NQ], F32, name=f"q_raw{o}", align_bytes=64) for o in range(PASSES)]
+        for o in range(PASSES):
+            nc.sync.dma_start(q_raw[o][:], q_hbm[o])
+        nc.sync.dma_start(offsets[:], offs)
         ks = sb.tile([P, PASSES, T // 4], I32, name="ks", align_bytes=64)
         cs = sb.tile([P, T // 4], I32, name="cs", align_bytes=64)
         warm = sb.tile([P, 8], F32, name="warm")
@@ -49,8 +51,8 @@ def tile_attend_neu_mix_topk_kernel(tc, qT, k_words, k_scales, c_words, c_scales
             )
         nc.scalar.activation(warm_out[:], warm[:], ACT.Sigmoid)
 
-        q_raw = sb.tile([P, PASSES, PACK, NQ], F32, name="q_raw", align_bytes=64)
-        nc.sync.dma_start(q_raw[:], qT[0].rearrange("(o p j) w -> p o j w", o=PASSES, j=PACK))
+        kw = sb.tile([P, T], I32, name="kw", align_bytes=64)
+        nc.sync.dma_start(kw[:], k_words[0].rearrange("p t b -> p (t b)").bitcast(I32))
         cw = [sb.tile([P, T], I32, name=f"cw{o}", align_bytes=64) for o in range(PASSES)]
         nc.sync.dma_start(cw[0][:], c_words[0].rearrange("p t b -> p (t b)").bitcast(I32))
         for quad in range(4):
@@ -62,21 +64,28 @@ def tile_attend_neu_mix_topk_kernel(tc, qT, k_words, k_scales, c_words, c_scales
         ksg = sb.tile([P, PASSES, N], U8, name="ksg", align_bytes=64)
         kwg = sb.tile([P, N], U32, name="kwg", align_bytes=64)
         k_codes = sb.tile([P, PASSES, N], U16, name="k_codes", align_bytes=64)
-        nc.vector.tensor_copy(kwg[:], kw[:].bitcast(U32).indirect(offsets[:]))
-        nc.vector.tensor_copy(ksg[:, 0, :], ks[:, 0, :].bitcast(U8).indirect(offsets[:]))
-        nc.vector.tensor_copy(k_codes[:], kwg[:].bitcast(U16).rearrange("p (n o) -> p o n", o=PASSES))
-        nc.vector.tensor_copy(ksg[:, 1, :], ks[:, 1, :].bitcast(U8).indirect(offsets[:]))
-
         q_bf = sb.tile([P, PASSES, NQ, PACK], BF16, name="q_bf", align_bytes=64)
-        for o in range(PASSES):
-            nc.scalar.activation(q_bf[:, o, :, :], q_raw[:, o, :, :].rearrange("p j w -> p w j"), ACT.Copy)
         q_codes = sb.tile([P, PASSES * NQ], U32, name="q_codes", align_bytes=64)
         q_scales = sb.tile([P, PASSES * NQ], U8, name="q_scales", align_bytes=64)
-        nc.vector.quantize_mx(
-            out=q_codes[:].bitcast(FP8X4),
-            scales=q_scales[:],
-            in_=q_bf[:].rearrange("p o w j -> p (o w j)"),
-        )
+        for o in range(PASSES):
+            nc.scalar.activation(q_bf[:, o, :, :], q_raw[o][:].rearrange("p j w -> p w j"), ACT.Copy)
+
+        def quantize(o):
+            cols = slice(o * NQ, (o + 1) * NQ)
+            nc.vector.quantize_mx(
+                out=q_codes[:, cols].bitcast(FP8X4),
+                scales=q_scales[:, cols],
+                in_=q_bf[:, o, :, :].rearrange("p w j -> p (w j)"),
+            )
+
+        for o in range(PASSES):
+            nc.vector.tensor_copy(ksg[:, o, :], ks[:, o, :].bitcast(U8).indirect(offsets[:]))
+        quantize(0)
+        nc.vector.tensor_copy(kwg[:], kw[:].bitcast(U32).indirect(offsets[:]))
+        quantize(1)
+        pairs = kwg[:].bitcast(U16).rearrange("p (n o) -> p o n", o=PASSES)
+        for o in range(PASSES):
+            nc.vector.tensor_copy(k_codes[:, o, :], pairs[:, o, :])
 
         a_ps = ps.tile([P, N], F32, name="a_ps")
         for o in range(PASSES):

@@ -20,54 +20,59 @@ P = 128
 PACK = 4
 PASSES = D // (P * PACK)
 HALF = N // 2
-C_ROW = 8
 
 
 def tile_attend_neu_mix_topk_kernel(tc, qT, k_words, k_scales, c_words, c_scales, offs, out):
     nc = tc.nc
     with ExitStack() as ctx:
         sb = ctx.enter_context(tc.tile_pool(name="sb", bufs=1))
+        pools = ctx.enter_context(tc.tile_pool(name="pools", bufs=2))
         ps = ctx.enter_context(tc.psum_pool(name="ps", bufs=1))
 
         offsets = sb.tile([P, N // 16], U16, name="offsets")
-
         q_hbm = qT[0].rearrange("(o p j) w -> o p j w", o=PASSES, j=PACK)
         q_raw = [sb.tile([P, PACK, NQ], F32, name=f"q_raw{o}", align_bytes=64) for o in range(PASSES)]
-        for o in range(PASSES):
-            nc.sync.dma_start(q_raw[o][:], q_hbm[o])
-        nc.sync.dma_start(offsets[:], offs)
-        ks = sb.tile([P, PASSES, T // 4], I32, name="ks", align_bytes=64)
+        ks = sb.tile([P, T // 4], I32, name="ks", align_bytes=64)
         cs = sb.tile([P, T // 4], I32, name="cs", align_bytes=64)
+        k_plane = sb.tile([P, PASSES, N // 4], I32, name="k_plane", align_bytes=64)
+        c_plane = sb.tile([P, PASSES, N // 4], I32, name="c_plane", align_bytes=64)
         warm = sb.tile([P, 8], F32, name="warm")
         warm_out = sb.tile([P, 8], F32, name="warm_out")
         nc.vector.memset(ks[:], 0)
-        nc.vector.memset(cs[:], 0)
         nc.vector.memset(warm[:], 0.0)
-        for quad in range(4):
-            rows = slice(4 * quad, 4 * quad + 4)
-            nc.sync.dma_start(
-                ks[32 * quad : 32 * quad + 4, :, :],
-                k_scales[:, rows, :].rearrange("o f t -> f o t").bitcast(I32),
-            )
+        nc.vector.memset(cs[:], 0)
+        nc.vector.memset(k_plane[:], 0)
+        nc.vector.memset(c_plane[:], 0)
         nc.scalar.activation(warm_out[:], warm[:], ACT.Sigmoid)
 
-        kw = sb.tile([P, T], I32, name="kw", align_bytes=64)
-        nc.sync.dma_start(kw[:], k_words[0].rearrange("p t b -> p (t b)").bitcast(I32))
-        cw = [sb.tile([P, T], I32, name=f"cw{o}", align_bytes=64) for o in range(PASSES)]
-        nc.sync.dma_start(cw[0][:], c_words[0].rearrange("p t b -> p (t b)").bitcast(I32))
-        for quad in range(4):
-            rows = slice(4 * quad, 4 * quad + 4)
-            first = 32 * quad + C_ROW
-            nc.sync.dma_start(cs[first : first + 8, :], c_scales[:, rows, :].bitcast(I32))
-        nc.sync.dma_start(cw[1][:], c_words[1].rearrange("p t b -> p (t b)").bitcast(I32))
+        def load_words(words, name):
+            tile = pools.tile([P, T], I32, name=name, tag="words", align_bytes=64)
+            nc.sync.dma_start(tile[:], words.rearrange("p t b -> p (t b)").bitcast(I32))
+            return tile
 
-        ksg = sb.tile([P, PASSES, N], U8, name="ksg", align_bytes=64)
-        kwg = sb.tile([P, N], U32, name="kwg", align_bytes=64)
-        k_codes = sb.tile([P, PASSES, N], U16, name="k_codes", align_bytes=64)
+        def load_scales(tile, scales):
+            nc.sync.dma_start(tile[0:P:4, :], scales.rearrange("o f t -> f o t").bitcast(I32))
+
+        def place(plane, rows):
+            for quad in range(4):
+                nc.scalar.dma_start(
+                    plane[32 * quad : 32 * quad + 4, :, :],
+                    rows[32 * quad : 32 * quad + 32 : 4, :].bitcast(I32),
+                )
+
+        nc.sync.dma_start(q_raw[0][:], q_hbm[0])
+        nc.sync.dma_start(offsets[:], offs)
+        load_scales(ks, k_scales)
+        kw = load_words(k_words[0], "kw")
+        nc.sync.dma_start(q_raw[1][:], q_hbm[1])
+        load_scales(cs, c_scales)
+        cw0 = load_words(c_words[0], "cw0")
+
         q_bf = sb.tile([P, PASSES, NQ, PACK], BF16, name="q_bf", align_bytes=64)
         q_codes = sb.tile([P, PASSES * NQ], U32, name="q_codes", align_bytes=64)
         q_scales = sb.tile([P, PASSES * NQ], U8, name="q_scales", align_bytes=64)
-        for o in range(PASSES):
+
+        def cast(o):
             nc.scalar.activation(q_bf[:, o, :, :], q_raw[o][:].rearrange("p j w -> p w j"), ACT.Copy)
 
         def quantize(o):
@@ -78,14 +83,23 @@ def tile_attend_neu_mix_topk_kernel(tc, qT, k_words, k_scales, c_words, c_scales
                 in_=q_bf[:, o, :, :].rearrange("p w j -> p (w j)"),
             )
 
-        for o in range(PASSES):
-            nc.vector.tensor_copy(ksg[:, o, :], ks[:, o, :].bitcast(U8).indirect(offsets[:]))
+        ksg = sb.tile([P, N], U8, name="ksg", align_bytes=64)
+        csg = sb.tile([P, N], U8, name="csg", align_bytes=64)
+        kwg = sb.tile([P, N], U32, name="kwg", align_bytes=64)
+        k_codes = sb.tile([P, PASSES, N], U16, name="k_codes", align_bytes=64)
+        cast(0)
+        nc.vector.tensor_copy(ksg[:], ks[:].bitcast(U8).indirect(offsets[:]))
+        place(k_plane, ksg)
         quantize(0)
         nc.vector.tensor_copy(kwg[:], kw[:].bitcast(U32).indirect(offsets[:]))
-        quantize(1)
+        cw = [cw0, load_words(c_words[1], "cw1")]
+        cast(1)
+        nc.vector.tensor_copy(csg[:], cs[:].bitcast(U8).indirect(offsets[:]))
+        place(c_plane, csg)
         pairs = kwg[:].bitcast(U16).rearrange("p (n o) -> p o n", o=PASSES)
         for o in range(PASSES):
             nc.vector.tensor_copy(k_codes[:, o, :], pairs[:, o, :])
+        quantize(1)
 
         a_ps = ps.tile([P, N], F32, name="a_ps")
         for o in range(PASSES):
@@ -95,7 +109,7 @@ def tile_attend_neu_mix_topk_kernel(tc, qT, k_words, k_scales, c_words, c_scales
                 lhsT=q_codes[:, cols].bitcast(FP8X4),
                 lhsT_scale=q_scales[:, cols],
                 rhs=k_codes[:, o, :].bitcast(FP4X4),
-                rhs_scale=ksg[:, o, :],
+                rhs_scale=k_plane[:, o, :].bitcast(U8),
                 start=(o == 0),
                 stop=(o == PASSES - 1),
             )
@@ -105,8 +119,6 @@ def tile_attend_neu_mix_topk_kernel(tc, qT, k_words, k_scales, c_words, c_scales
         z_ps = [ps.tile([P, N], F32, name=f"z_ps{h}") for h in range(2)]
         cwg = [sb.tile([P, N], U32, name=f"cwg{o}", align_bytes=64) for o in range(PASSES)]
         nc.vector.tensor_copy(cwg[0][:], cw[0][:].bitcast(U32).indirect(offsets[:]))
-        csg = sb.tile([P, N], U8, name="csg", align_bytes=64)
-        nc.vector.tensor_copy(csg[:], cs[:].bitcast(U8).indirect(offsets[:]))
         for h in range(2):
             slots = slice(h * HALF, (h + 1) * HALF)
             nc.vector.tensor_copy(
@@ -122,7 +134,7 @@ def tile_attend_neu_mix_topk_kernel(tc, qT, k_words, k_scales, c_words, c_scales
                     lhsT=q_codes[:, cols].bitcast(FP8X4),
                     lhsT_scale=q_scales[:, cols],
                     rhs=cwg[o][:, slots].bitcast(FP8X4),
-                    rhs_scale=csg[C_ROW + 4 * o :, slots],
+                    rhs_scale=c_plane[:, o, :].bitcast(U8)[:, slots],
                     start=(o == 0),
                     stop=(o == PASSES - 1),
                 )

@@ -26,54 +26,52 @@ def tile_attend_neu_mix_topk_kernel(tc, qT, k_words, k_scales, c_words, c_scales
     nc = tc.nc
     with ExitStack() as ctx:
         sb = ctx.enter_context(tc.tile_pool(name="sb", bufs=1))
-        pools = ctx.enter_context(tc.tile_pool(name="pools", bufs=2))
         ps = ctx.enter_context(tc.psum_pool(name="ps", bufs=1))
 
         offsets = sb.tile([P, N // 16], U16, name="offsets")
-        q_hbm = qT[0].rearrange("(o p j) w -> o p j w", o=PASSES, j=PACK)
-        q_raw = [sb.tile([P, PACK, NQ], F32, name=f"q_raw{o}", align_bytes=64) for o in range(PASSES)]
+        q_hbm = qT[0].rearrange("(o p j) w -> p o (j w)", o=PASSES, j=PACK)
+        q_raw = sb.tile([P, PASSES, PACK * NQ], F32, name="q_raw", align_bytes=64)
         ks = sb.tile([P, T // 4], I32, name="ks", align_bytes=64)
         cs = sb.tile([P, T // 4], I32, name="cs", align_bytes=64)
         k_plane = sb.tile([P, PASSES, N // 4], I32, name="k_plane", align_bytes=64)
-        c_plane = sb.tile([P, PASSES, N // 4], I32, name="c_plane", align_bytes=64)
         warm = sb.tile([P, 8], F32, name="warm")
         warm_out = sb.tile([P, 8], F32, name="warm_out")
-        nc.vector.memset(ks[:], 0)
-        nc.vector.memset(warm[:], 0.0)
         nc.vector.memset(cs[:], 0)
+        nc.vector.memset(ks[0:64, :], 0)
+        nc.vector.memset(ks[96:P, :], 0)
+        nc.vector.memset(warm[:], 0.0)
         nc.vector.memset(k_plane[:], 0)
-        nc.vector.memset(c_plane[:], 0)
-        nc.scalar.activation(warm_out[:], warm[:], ACT.Sigmoid)
 
         def load_words(words, name):
-            tile = pools.tile([P, T], I32, name=name, tag="words", align_bytes=64)
+            tile = sb.tile([P, T], I32, name=name, align_bytes=64)
             nc.sync.dma_start(tile[:], words.rearrange("p t b -> p (t b)").bitcast(I32))
             return tile
-
-        def load_scales(tile, scales):
-            nc.sync.dma_start(tile[0:P:4, :], scales.rearrange("o f t -> f o t").bitcast(I32))
 
         def place(plane, rows):
             for quad in range(4):
                 nc.scalar.dma_start(
                     plane[32 * quad : 32 * quad + 4, :, :],
-                    rows[32 * quad : 32 * quad + 32 : 4, :].bitcast(I32),
+                    rows[64 + 8 * quad : 72 + 8 * quad, :].bitcast(I32),
                 )
 
-        nc.sync.dma_start(q_raw[0][:], q_hbm[0])
         nc.sync.dma_start(offsets[:], offs)
-        load_scales(ks, k_scales)
+        nc.sync.dma_start(q_raw[:], q_hbm)
+        nc.scalar.dma_start(ks[64:96, :], k_scales.rearrange("o f t -> f o t").bitcast(I32))
+        for quad in range(4):
+            nc.sync.dma_start(
+                cs[32 * quad + 4 : 32 * quad + 12, :],
+                c_scales[:, 4 * quad : 4 * quad + 4, :].bitcast(I32),
+            )
         kw = load_words(k_words[0], "kw")
-        nc.sync.dma_start(q_raw[1][:], q_hbm[1])
-        load_scales(cs, c_scales)
-        cw0 = load_words(c_words[0], "cw0")
+        cw = [load_words(c_words[o], f"cw{o}") for o in range(PASSES)]
+        nc.scalar.activation(warm_out[:], warm[:], ACT.Sigmoid)
 
         q_bf = sb.tile([P, PASSES, NQ, PACK], BF16, name="q_bf", align_bytes=64)
         q_codes = sb.tile([P, PASSES * NQ], U32, name="q_codes", align_bytes=64)
         q_scales = sb.tile([P, PASSES * NQ], U8, name="q_scales", align_bytes=64)
 
         def cast(o):
-            nc.scalar.activation(q_bf[:, o, :, :], q_raw[o][:].rearrange("p j w -> p w j"), ACT.Copy)
+            nc.scalar.activation(q_bf[:, o, :, :], q_raw[:, o, :].rearrange("p (j w) -> p w j", j=PACK), ACT.Copy)
 
         def quantize(o):
             cols = slice(o * NQ, (o + 1) * NQ)
@@ -87,19 +85,17 @@ def tile_attend_neu_mix_topk_kernel(tc, qT, k_words, k_scales, c_words, c_scales
         csg = sb.tile([P, N], U8, name="csg", align_bytes=64)
         kwg = sb.tile([P, N], U32, name="kwg", align_bytes=64)
         k_codes = sb.tile([P, PASSES, N], U16, name="k_codes", align_bytes=64)
-        cast(0)
         nc.vector.tensor_copy(ksg[:], ks[:].bitcast(U8).indirect(offsets[:]))
         place(k_plane, ksg)
-        quantize(0)
-        nc.vector.tensor_copy(kwg[:], kw[:].bitcast(U32).indirect(offsets[:]))
-        cw = [cw0, load_words(c_words[1], "cw1")]
-        cast(1)
         nc.vector.tensor_copy(csg[:], cs[:].bitcast(U8).indirect(offsets[:]))
-        place(c_plane, csg)
+        cast(0)
+        cast(1)
+        quantize(0)
+        quantize(1)
+        nc.vector.tensor_copy(kwg[:], kw[:].bitcast(U32).indirect(offsets[:]))
         pairs = kwg[:].bitcast(U16).rearrange("p (n o) -> p o n", o=PASSES)
         for o in range(PASSES):
             nc.vector.tensor_copy(k_codes[:, o, :], pairs[:, o, :])
-        quantize(1)
 
         a_ps = ps.tile([P, N], F32, name="a_ps")
         for o in range(PASSES):
@@ -134,7 +130,7 @@ def tile_attend_neu_mix_topk_kernel(tc, qT, k_words, k_scales, c_words, c_scales
                     lhsT=q_codes[:, cols].bitcast(FP8X4),
                     lhsT_scale=q_scales[:, cols],
                     rhs=cwg[o][:, slots].bitcast(FP8X4),
-                    rhs_scale=c_plane[:, o, :].bitcast(U8)[:, slots],
+                    rhs_scale=csg[4 + 4 * o : P, slots],
                     start=(o == 0),
                     stop=(o == PASSES - 1),
                 )

@@ -34,36 +34,33 @@ def tile_attend_neu_mix_topk_kernel(tc, qT, k_words, k_scales, c_words, c_scales
         ks = sb.tile([P, T // 4], I32, name="ks", align_bytes=64)
         cs = sb.tile([P, T // 4], I32, name="cs", align_bytes=64)
         k_plane = sb.tile([P, PASSES, N // 4], I32, name="k_plane", align_bytes=64)
+        c_plane = sb.tile([P, PASSES, N // 4], I32, name="c_plane", align_bytes=64)
         warm = sb.tile([P, 8], F32, name="warm")
         warm_out = sb.tile([P, 8], F32, name="warm_out")
         nc.vector.memset(cs[:], 0)
-        nc.vector.memset(ks[0:64, :], 0)
-        nc.vector.memset(ks[96:P, :], 0)
+        nc.vector.memset(ks[0:96, :], 0)
         nc.vector.memset(warm[:], 0.0)
-        nc.vector.memset(k_plane[:], 0)
+        nc.gpsimd.memset(k_plane[:], 0)
+        nc.gpsimd.memset(c_plane[:], 0)
 
         def load_words(words, name):
             tile = sb.tile([P, T], I32, name=name, align_bytes=64)
             nc.sync.dma_start(tile[:], words.rearrange("p t b -> p (t b)").bitcast(I32))
             return tile
 
-        def place(plane, rows):
+        def place(queue, plane, rows, first, step):
             for quad in range(4):
-                nc.scalar.dma_start(
+                queue.dma_start(
                     plane[32 * quad : 32 * quad + 4, :, :],
-                    rows[64 + 8 * quad : 72 + 8 * quad, :].bitcast(I32),
+                    rows[first + 8 * step * quad : first + 8 * step * (quad + 1) : step, :].bitcast(I32),
                 )
 
         nc.sync.dma_start(offsets[:], offs)
+        nc.sync.dma_start(ks[96:P, :], k_scales.rearrange("o f t -> f o t").bitcast(I32))
         nc.sync.dma_start(q_raw[:], q_hbm)
-        nc.scalar.dma_start(ks[64:96, :], k_scales.rearrange("o f t -> f o t").bitcast(I32))
-        for quad in range(4):
-            nc.sync.dma_start(
-                cs[32 * quad + 4 : 32 * quad + 12, :],
-                c_scales[:, 4 * quad : 4 * quad + 4, :].bitcast(I32),
-            )
+        nc.sync.dma_start(cs[0:P:4, :], c_scales.rearrange("o f t -> f o t").bitcast(I32))
         kw = load_words(k_words[0], "kw")
-        cw = [load_words(c_words[o], f"cw{o}") for o in range(PASSES)]
+        cw0 = load_words(c_words[0], "cw0")
         nc.scalar.activation(warm_out[:], warm[:], ACT.Sigmoid)
 
         q_bf = sb.tile([P, PASSES, NQ, PACK], BF16, name="q_bf", align_bytes=64)
@@ -86,8 +83,10 @@ def tile_attend_neu_mix_topk_kernel(tc, qT, k_words, k_scales, c_words, c_scales
         kwg = sb.tile([P, N], U32, name="kwg", align_bytes=64)
         k_codes = sb.tile([P, PASSES, N], U16, name="k_codes", align_bytes=64)
         nc.vector.tensor_copy(ksg[:], ks[:].bitcast(U8).indirect(offsets[:]))
-        place(k_plane, ksg)
+        place(nc.sync, k_plane, ksg, 96, 1)
+        cw = [cw0, load_words(c_words[1], "cw1")]
         nc.vector.tensor_copy(csg[:], cs[:].bitcast(U8).indirect(offsets[:]))
+        place(nc.sync, c_plane, csg, 0, 4)
         cast(0)
         cast(1)
         quantize(0)
@@ -130,7 +129,7 @@ def tile_attend_neu_mix_topk_kernel(tc, qT, k_words, k_scales, c_words, c_scales
                     lhsT=q_codes[:, cols].bitcast(FP8X4),
                     lhsT_scale=q_scales[:, cols],
                     rhs=cwg[o][:, slots].bitcast(FP8X4),
-                    rhs_scale=csg[4 + 4 * o : P, slots],
+                    rhs_scale=c_plane[:, o, :].bitcast(U8)[:, slots],
                     start=(o == 0),
                     stop=(o == PASSES - 1),
                 )

@@ -37,9 +37,10 @@ def tile_attend_neu_mix_topk_kernel(tc, qT, k_words, k_scales, c_words, c_scales
         c_plane = sb.tile([P, PASSES, N // 4], I32, name="c_plane", align_bytes=64)
         warm = sb.tile([P, 8], F32, name="warm")
         warm_out = sb.tile([P, 8], F32, name="warm_out")
-        nc.vector.memset(cs[:], 0)
-        nc.vector.memset(ks[0:96, :], 0)
         nc.vector.memset(warm[:], 0.0)
+        nc.vector.memset(ks[0:96, :], 0)
+        nc.vector.memset(cs[64:P, :], 0)
+        nc.gpsimd.memset(cs[32:64, :], 0)
         nc.gpsimd.memset(k_plane[:], 0)
         nc.gpsimd.memset(c_plane[:], 0)
 
@@ -48,19 +49,18 @@ def tile_attend_neu_mix_topk_kernel(tc, qT, k_words, k_scales, c_words, c_scales
             nc.sync.dma_start(tile[:], words.rearrange("p t b -> p (t b)").bitcast(I32))
             return tile
 
-        def place(queue, plane, rows, first, step):
-            for quad in range(4):
-                queue.dma_start(
-                    plane[32 * quad : 32 * quad + 4, :, :],
-                    rows[first + 8 * step * quad : first + 8 * step * (quad + 1) : step, :].bitcast(I32),
+        def place(plane, first, rows, start, quads):
+            for quad in quads:
+                nc.sync.dma_start(
+                    plane[32 * quad + first : 32 * quad + first + 4, :, :],
+                    rows[start + 8 * quad : start + 8 * quad + 8, :].bitcast(I32),
                 )
 
         nc.sync.dma_start(offsets[:], offs)
         nc.sync.dma_start(ks[96:P, :], k_scales.rearrange("o f t -> f o t").bitcast(I32))
+        nc.sync.dma_start(cs[0:32, :], c_scales.rearrange("o f t -> f o t").bitcast(I32))
         nc.sync.dma_start(q_raw[:], q_hbm)
-        nc.sync.dma_start(cs[0:P:4, :], c_scales.rearrange("o f t -> f o t").bitcast(I32))
         kw = load_words(k_words[0], "kw")
-        cw0 = load_words(c_words[0], "cw0")
         nc.scalar.activation(warm_out[:], warm[:], ACT.Sigmoid)
 
         q_bf = sb.tile([P, PASSES, NQ, PACK], BF16, name="q_bf", align_bytes=64)
@@ -83,10 +83,12 @@ def tile_attend_neu_mix_topk_kernel(tc, qT, k_words, k_scales, c_words, c_scales
         kwg = sb.tile([P, N], U32, name="kwg", align_bytes=64)
         k_codes = sb.tile([P, PASSES, N], U16, name="k_codes", align_bytes=64)
         nc.vector.tensor_copy(ksg[:], ks[:].bitcast(U8).indirect(offsets[:]))
-        place(nc.sync, k_plane, ksg, 96, 1)
-        cw = [cw0, load_words(c_words[1], "cw1")]
+        place(k_plane, 0, ksg, 96, range(2))
+        cw0 = load_words(c_words[0], "cw0")
+        place(k_plane, 0, ksg, 96, range(2, 4))
         nc.vector.tensor_copy(csg[:], cs[:].bitcast(U8).indirect(offsets[:]))
-        place(nc.sync, c_plane, csg, 0, 4)
+        place(c_plane, 4, csg, 0, range(4))
+        cw = [cw0, load_words(c_words[1], "cw1")]
         cast(0)
         cast(1)
         quantize(0)
@@ -129,7 +131,7 @@ def tile_attend_neu_mix_topk_kernel(tc, qT, k_words, k_scales, c_words, c_scales
                     lhsT=q_codes[:, cols].bitcast(FP8X4),
                     lhsT_scale=q_scales[:, cols],
                     rhs=cwg[o][:, slots].bitcast(FP8X4),
-                    rhs_scale=c_plane[:, o, :].bitcast(U8)[:, slots],
+                    rhs_scale=c_plane[4:P, o, :].bitcast(U8)[:, slots],
                     start=(o == 0),
                     stop=(o == PASSES - 1),
                 )

@@ -35,9 +35,6 @@ def tile_attend_neu_mix_topk_kernel(tc, qT, k_words, k_scales, c_words, c_scales
         cs = sb.tile([P, T // 4], I32, name="cs", align_bytes=64)
         k_plane = sb.tile([P, PASSES, N // 4], I32, name="k_plane", align_bytes=64)
         c_plane = sb.tile([P, PASSES, N // 4], I32, name="c_plane", align_bytes=64)
-        warm = sb.tile([P, 8], F32, name="warm")
-        warm_out = sb.tile([P, 8], F32, name="warm_out")
-        nc.vector.memset(warm[:], 0.0)
         nc.vector.memset(ks[0:96, :], 0)
         nc.vector.memset(cs[64:P, :], 0)
         nc.gpsimd.memset(cs[32:64, :], 0)
@@ -61,14 +58,13 @@ def tile_attend_neu_mix_topk_kernel(tc, qT, k_words, k_scales, c_words, c_scales
         nc.sync.dma_start(cs[0:32, :], c_scales.rearrange("o f t -> f o t").bitcast(I32))
         nc.sync.dma_start(q_raw[:], q_hbm)
         kw = load_words(k_words[0], "kw")
-        nc.scalar.activation(warm_out[:], warm[:], ACT.Sigmoid)
 
         q_bf = sb.tile([P, PASSES, NQ, PACK], BF16, name="q_bf", align_bytes=64)
         q_codes = sb.tile([P, PASSES * NQ], U32, name="q_codes", align_bytes=64)
         q_scales = sb.tile([P, PASSES * NQ], U8, name="q_scales", align_bytes=64)
 
         def cast(o):
-            nc.scalar.activation(q_bf[:, o, :, :], q_raw[:, o, :].rearrange("p (j w) -> p w j", j=PACK), ACT.Copy)
+            nc.scalar.copy(q_bf[:, o, :, :], q_raw[:, o, :].rearrange("p (j w) -> p w j", j=PACK))
 
         def quantize(o):
             cols = slice(o * NQ, (o + 1) * NQ)
@@ -113,7 +109,8 @@ def tile_attend_neu_mix_topk_kernel(tc, qT, k_words, k_scales, c_words, c_scales
         gate = sb.tile([P, N], F32, name="gate")
         nc.scalar.activation(gate[:], a_ps[:], ACT.Sigmoid)
 
-        z_ps = [ps.tile([P, N], F32, name=f"z_ps{h}") for h in range(2)]
+        pieces = [slice(0, HALF), slice(HALF, HALF + P), slice(HALF + P, N)]
+        z_ps = [ps.tile([P, N], F32, name=f"z_ps{h}") for h in range(len(pieces))]
         cwg = [sb.tile([P, N], U32, name=f"cwg{o}", align_bytes=64) for o in range(PASSES)]
         nc.vector.tensor_copy(cwg[0][:], cw[0][:].bitcast(U32).indirect(offsets[:]))
         for h in range(2):
@@ -124,10 +121,9 @@ def tile_attend_neu_mix_topk_kernel(tc, qT, k_words, k_scales, c_words, c_scales
             )
         for o in range(PASSES):
             cols = slice(o * NQ, (o + 1) * NQ)
-            for h in range(2):
-                slots = slice(h * HALF, (h + 1) * HALF)
+            for h, slots in enumerate(pieces):
                 nc.tensor.matmul_mx(
-                    out=z_ps[h][:, :HALF],
+                    out=z_ps[h][:, slots],
                     lhsT=q_codes[:, cols].bitcast(FP8X4),
                     lhsT_scale=q_scales[:, cols],
                     rhs=cwg[o][:, slots].bitcast(FP8X4),
@@ -136,7 +132,6 @@ def tile_attend_neu_mix_topk_kernel(tc, qT, k_words, k_scales, c_words, c_scales
                     stop=(o == PASSES - 1),
                 )
         res = sb.tile([P, N], F32, name="res")
-        for h in range(2):
-            slots = slice(h * HALF, (h + 1) * HALF)
-            nc.vector.tensor_tensor(res[:, slots], z_ps[h][:, :HALF], gate[:, slots], MULT)
+        for h, slots in enumerate(pieces):
+            nc.vector.tensor_tensor(res[:, slots], z_ps[h][:, slots], gate[:, slots], MULT)
             nc.sync.dma_start(out[0][:, slots], res[:, slots])

@@ -46,8 +46,8 @@ def tile_attend_neu_mix_topk_kernel(tc, qT, k_words, k_scales, c_words, c_scales
             nc.sync.dma_start(tile[:], words.rearrange("p t b -> p (t b)").bitcast(I32))
             return tile
 
-        def place(plane, first, rows, start, quads):
-            for quad in quads:
+        def place(plane, first, rows, start):
+            for quad in range(4):
                 nc.sync.dma_start(
                     plane[32 * quad + first : 32 * quad + first + 4, :, :],
                     rows[start + 8 * quad : start + 8 * quad + 8, :].bitcast(I32),
@@ -78,13 +78,12 @@ def tile_attend_neu_mix_topk_kernel(tc, qT, k_words, k_scales, c_words, c_scales
         csg = sb.tile([P, N], U8, name="csg", align_bytes=64)
         kwg = sb.tile([P, N], U32, name="kwg", align_bytes=64)
         k_codes = sb.tile([P, PASSES, N], U16, name="k_codes", align_bytes=64)
-        nc.vector.tensor_copy(ksg[:], ks[:].bitcast(U8).indirect(offsets[:]))
-        place(k_plane, 0, ksg, 96, range(2))
         cw0 = load_words(c_words[0], "cw0")
-        place(k_plane, 0, ksg, 96, range(2, 4))
-        nc.vector.tensor_copy(csg[:], cs[:].bitcast(U8).indirect(offsets[:]))
-        place(c_plane, 4, csg, 0, range(4))
+        nc.vector.tensor_copy(ksg[:], ks[:].bitcast(U8).indirect(offsets[:]))
+        place(k_plane, 0, ksg, 96)
         cw = [cw0, load_words(c_words[1], "cw1")]
+        nc.vector.tensor_copy(csg[:], cs[:].bitcast(U8).indirect(offsets[:]))
+        place(c_plane, 4, csg, 0)
         cast(0)
         cast(1)
         quantize(0)

@@ -37,9 +37,9 @@ def tile_attend_neu_mix_topk_kernel(tc, qT, k_words, k_scales, c_words, c_scales
         c_plane = sb.tile([P, PASSES, N // 4], I32, name="c_plane", align_bytes=64)
         nc.vector.memset(ks[0:96, :], 0)
         nc.vector.memset(cs[64:P, :], 0)
-        nc.gpsimd.memset(cs[32:64, :], 0)
-        nc.gpsimd.memset(k_plane[:], 0)
-        nc.gpsimd.memset(c_plane[:], 0)
+        nc.vector.memset(cs[32:64, :], 0)
+        nc.vector.memset(k_plane[:], 0)
+        nc.vector.memset(c_plane[:], 0)
 
         def load_words(words, name):
             tile = sb.tile([P, T], I32, name=name, align_bytes=64)
@@ -66,14 +66,6 @@ def tile_attend_neu_mix_topk_kernel(tc, qT, k_words, k_scales, c_words, c_scales
         def cast(o):
             nc.scalar.copy(q_bf[:, o, :, :], q_raw[:, o, :].rearrange("p (j w) -> p w j", j=PACK))
 
-        def quantize(o):
-            cols = slice(o * NQ, (o + 1) * NQ)
-            nc.vector.quantize_mx(
-                out=q_codes[:, cols].bitcast(FP8X4),
-                scales=q_scales[:, cols],
-                in_=q_bf[:, o, :, :].rearrange("p w j -> p (w j)"),
-            )
-
         ksg = sb.tile([P, N], U8, name="ksg", align_bytes=64)
         csg = sb.tile([P, N], U8, name="csg", align_bytes=64)
         kwg = sb.tile([P, N], U32, name="kwg", align_bytes=64)
@@ -86,12 +78,14 @@ def tile_attend_neu_mix_topk_kernel(tc, qT, k_words, k_scales, c_words, c_scales
         place(c_plane, 4, csg, 0)
         cast(0)
         cast(1)
-        quantize(0)
-        quantize(1)
+        nc.vector.quantize_mx(
+            out=q_codes[:].bitcast(FP8X4),
+            scales=q_scales[:],
+            in_=q_bf[:].rearrange("p o w j -> p (o w j)"),
+        )
         nc.vector.tensor_copy(kwg[:], kw[:].bitcast(U32).indirect(offsets[:]))
         pairs = kwg[:].bitcast(U16).rearrange("p (n o) -> p o n", o=PASSES)
-        for o in range(PASSES):
-            nc.vector.tensor_copy(k_codes[:, o, :], pairs[:, o, :])
+        nc.vector.tensor_copy(k_codes[:], pairs)
 
         a_ps = ps.tile([P, N], F32, name="a_ps")
         for o in range(PASSES):

@@ -35,9 +35,8 @@ def tile_attend_neu_mix_topk_kernel(tc, qT, k_words, k_scales, c_words, c_scales
         cs = sb.tile([P, T // 4], I32, name="cs", align_bytes=64)
         k_plane = sb.tile([P, PASSES, N // 4], I32, name="k_plane", align_bytes=64)
         c_plane = sb.tile([P, PASSES, N // 4], I32, name="c_plane", align_bytes=64)
-        nc.vector.memset(ks[0:96, :], 0)
-        nc.vector.memset(cs[64:P, :], 0)
-        nc.vector.memset(cs[32:64, :], 0)
+        nc.vector.memset(ks[:], 0)
+        nc.vector.memset(cs[:], 0)
         nc.vector.memset(k_plane[:], 0)
         nc.vector.memset(c_plane[:], 0)
 
@@ -46,17 +45,17 @@ def tile_attend_neu_mix_topk_kernel(tc, qT, k_words, k_scales, c_words, c_scales
             nc.sync.dma_start(tile[:], words.rearrange("p t b -> p (t b)").bitcast(I32))
             return tile
 
-        def place(plane, first, rows, start):
+        def place(plane, first, rows):
             for quad in range(4):
                 nc.sync.dma_start(
                     plane[32 * quad + first : 32 * quad + first + 4, :, :],
-                    rows[start + 8 * quad : start + 8 * quad + 8, :].bitcast(I32),
+                    rows[32 + 16 * quad : 32 + 16 * quad + 16 : 2, :].bitcast(I32),
                 )
 
         nc.sync.dma_start(offsets[:], offs)
-        nc.sync.dma_start(ks[96:P, :], k_scales.rearrange("o f t -> f o t").bitcast(I32))
-        nc.sync.dma_start(cs[0:32, :], c_scales.rearrange("o f t -> f o t").bitcast(I32))
         nc.sync.dma_start(q_raw[:], q_hbm)
+        nc.sync.dma_start(ks[32:96:2, :], k_scales.rearrange("o f t -> f o t").bitcast(I32))
+        nc.sync.dma_start(cs[32:96:2, :], c_scales.rearrange("o f t -> f o t").bitcast(I32))
         kw = load_words(k_words[0], "kw")
 
         q_bf = sb.tile([P, PASSES, NQ, PACK], BF16, name="q_bf", align_bytes=64)
@@ -72,10 +71,10 @@ def tile_attend_neu_mix_topk_kernel(tc, qT, k_words, k_scales, c_words, c_scales
         k_codes = sb.tile([P, PASSES, N], U16, name="k_codes", align_bytes=64)
         cw0 = load_words(c_words[0], "cw0")
         nc.vector.tensor_copy(ksg[:], ks[:].bitcast(U8).indirect(offsets[:]))
-        place(k_plane, 0, ksg, 96)
+        place(k_plane, 0, ksg)
         cw = [cw0, load_words(c_words[1], "cw1")]
         nc.vector.tensor_copy(csg[:], cs[:].bitcast(U8).indirect(offsets[:]))
-        place(c_plane, 4, csg, 0)
+        place(c_plane, 4, csg)
         cast(0)
         cast(1)
         nc.vector.quantize_mx(

@@ -46,7 +46,7 @@ def tile_attend_neu_mix_topk_kernel(tc, qT, k_words, k_scales, c_words, c_scales
             return tile
 
         def place(plane, first, rows):
-            for quad in range(4):
+            for quad in (0, 2, 1, 3):
                 nc.sync.dma_start(
                     plane[32 * quad + first : 32 * quad + first + 4, :, :],
                     rows[32 + 16 * quad : 32 + 16 * quad + 16 : 2, :].bitcast(I32),

@@ -52,8 +52,8 @@ def tile_attend_neu_mix_topk_kernel(tc, qT, k_words, k_scales, c_words, c_scales
                     rows[32 + 16 * quad : 32 + 16 * quad + 16 : 2, :].bitcast(I32),
                 )
 
-        nc.sync.dma_start(offsets[:], offs)
         nc.sync.dma_start(q_raw[:], q_hbm)
+        nc.sync.dma_start(offsets[:], offs)
         nc.sync.dma_start(ks[32:96:2, :], k_scales.rearrange("o f t -> f o t").bitcast(I32))
         nc.sync.dma_start(cs[32:96:2, :], c_scales.rearrange("o f t -> f o t").bitcast(I32))
         kw = load_words(k_words[0], "kw")

@@ -30,7 +30,7 @@ def tile_attend_neu_mix_topk_kernel(tc, qT, k_words, k_scales, c_words, c_scales
 
         offsets = sb.tile([P, N // 16], U16, name="offsets")
         q_hbm = qT[0].rearrange("(o p j) w -> p o (j w)", o=PASSES, j=PACK)
-        q_raw = sb.tile([P, PASSES, PACK * NQ], F32, name="q_raw", align_bytes=64)
+        q_raw = [sb.tile([P, PACK * NQ], F32, name=f"q_raw{o}", align_bytes=64) for o in range(PASSES)]
         ks = sb.tile([P, T // 4], I32, name="ks", align_bytes=64)
         cs = sb.tile([P, T // 4], I32, name="cs", align_bytes=64)
         k_plane = sb.tile([P, PASSES, N // 4], I32, name="k_plane", align_bytes=64)
@@ -52,9 +52,11 @@ def tile_attend_neu_mix_topk_kernel(tc, qT, k_words, k_scales, c_words, c_scales
                     rows[32 + 16 * quad : 32 + 16 * quad + 16 : 2, :].bitcast(I32),
                 )
 
-        nc.sync.dma_start(q_raw[:], q_hbm)
+        for o in range(PASSES):
+            nc.sync.dma_start(q_raw[o][:], q_hbm[:, o, :])
         nc.sync.dma_start(offsets[:], offs)
-        nc.sync.dma_start(ks[32:96:2, :], k_scales.rearrange("o f t -> f o t").bitcast(I32))
+        for o in range(PASSES):
+            nc.sync.dma_start(ks[32 + 2 * o : 96 : 4, :], k_scales[o].bitcast(I32))
         nc.sync.dma_start(cs[32:96:2, :], c_scales.rearrange("o f t -> f o t").bitcast(I32))
         kw = load_words(k_words[0], "kw")
 
@@ -63,7 +65,7 @@ def tile_attend_neu_mix_topk_kernel(tc, qT, k_words, k_scales, c_words, c_scales
         q_scales = sb.tile([P, PASSES * NQ], U8, name="q_scales", align_bytes=64)
 
         def cast(o):
-            nc.scalar.copy(q_bf[:, o, :, :], q_raw[:, o, :].rearrange("p (j w) -> p w j", j=PACK))
+            nc.scalar.copy(q_bf[:, o, :, :], q_raw[o][:].rearrange("p (j w) -> p w j", j=PACK))
 
         ksg = sb.tile([P, N], U8, name="ksg", align_bytes=64)
         csg = sb.tile([P, N], U8, name="csg", align_bytes=64)
@@ -101,7 +103,7 @@ def tile_attend_neu_mix_topk_kernel(tc, qT, k_words, k_scales, c_words, c_scales
         gate = sb.tile([P, N], F32, name="gate")
         nc.scalar.activation(gate[:], a_ps[:], ACT.Sigmoid)
 
-        pieces = [slice(0, HALF), slice(HALF, HALF + P), slice(HALF + P, N)]
+        pieces = [slice(c, c + P) for c in range(0, N, P)]
         z_ps = [ps.tile([P, N], F32, name=f"z_ps{h}") for h in range(len(pieces))]
         cwg = [sb.tile([P, N], U32, name=f"cwg{o}", align_bytes=64) for o in range(PASSES)]
         nc.vector.tensor_copy(cwg[0][:], cw[0][:].bitcast(U32).indirect(offsets[:]))
@@ -111,9 +113,9 @@ def tile_attend_neu_mix_topk_kernel(tc, qT, k_words, k_scales, c_words, c_scales
                 cwg[1][:, slots],
                 cw[1][:].bitcast(U32).indirect(offsets[:, h * HALF // 16 : (h + 1) * HALF // 16]),
             )
-        for o in range(PASSES):
-            cols = slice(o * NQ, (o + 1) * NQ)
-            for h, slots in enumerate(pieces):
+        for h, slots in enumerate(pieces):
+            for o in range(PASSES):
+                cols = slice(o * NQ, (o + 1) * NQ)
                 nc.tensor.matmul_mx(
                     out=z_ps[h][:, slots],
                     lhsT=q_codes[:, cols].bitcast(FP8X4),

@@ -30,18 +30,18 @@ def tile_attend_neu_mix_topk_kernel(tc, qT, k_words, k_scales, c_words, c_scales
 
         offsets = sb.tile([P, N // 16], U16, name="offsets")
         q_hbm = qT[0].rearrange("(o p j) w -> p o (j w)", o=PASSES, j=PACK)
-        q_raw = [sb.tile([P, PACK * NQ], F32, name=f"q_raw{o}", align_bytes=64) for o in range(PASSES)]
-        ks = sb.tile([P, T // 4], I32, name="ks", align_bytes=64)
-        cs = sb.tile([P, T // 4], I32, name="cs", align_bytes=64)
-        k_plane = sb.tile([P, PASSES, N // 4], I32, name="k_plane", align_bytes=64)
-        c_plane = sb.tile([P, PASSES, N // 4], I32, name="c_plane", align_bytes=64)
+        q_raw = [sb.tile([P, PACK * NQ], F32, name=f"q_raw{o}", align_bytes=256) for o in range(PASSES)]
+        ks = sb.tile([P, T // 4], I32, name="ks", align_bytes=256)
+        cs = sb.tile([P, T // 4], I32, name="cs", align_bytes=256)
+        k_plane = sb.tile([P, PASSES, N // 4], I32, name="k_plane", align_bytes=256)
+        c_plane = sb.tile([P, PASSES, N // 4], I32, name="c_plane", align_bytes=256)
         nc.vector.memset(ks[:], 0)
         nc.vector.memset(cs[:], 0)
         nc.vector.memset(k_plane[:], 0)
         nc.vector.memset(c_plane[:], 0)
 
         def load_words(words, name):
-            tile = sb.tile([P, T], I32, name=name, align_bytes=64)
+            tile = sb.tile([P, T], I32, name=name, align_bytes=256)
             nc.sync.dma_start(tile[:], words.rearrange("p t b -> p (t b)").bitcast(I32))
             return tile
 
@@ -60,17 +60,17 @@ def tile_attend_neu_mix_topk_kernel(tc, qT, k_words, k_scales, c_words, c_scales
         nc.sync.dma_start(cs[32:96:2, :], c_scales.rearrange("o f t -> f o t").bitcast(I32))
         kw = load_words(k_words[0], "kw")
 
-        q_bf = sb.tile([P, PASSES, NQ, PACK], BF16, name="q_bf", align_bytes=64)
-        q_codes = sb.tile([P, PASSES * NQ], U32, name="q_codes", align_bytes=64)
-        q_scales = sb.tile([P, PASSES * NQ], U8, name="q_scales", align_bytes=64)
+        q_bf = sb.tile([P, PASSES, NQ, PACK], BF16, name="q_bf", align_bytes=256)
+        q_codes = sb.tile([P, PASSES * NQ], U32, name="q_codes", align_bytes=256)
+        q_scales = sb.tile([P, PASSES * NQ], U8, name="q_scales", align_bytes=256)
 
         def cast(o):
             nc.scalar.copy(q_bf[:, o, :, :], q_raw[o][:].rearrange("p (j w) -> p w j", j=PACK))
 
-        ksg = sb.tile([P, N], U8, name="ksg", align_bytes=64)
-        csg = sb.tile([P, N], U8, name="csg", align_bytes=64)
-        kwg = sb.tile([P, N], U32, name="kwg", align_bytes=64)
-        k_codes = sb.tile([P, PASSES, N], U16, name="k_codes", align_bytes=64)
+        ksg = sb.tile([P, N], U8, name="ksg", align_bytes=256)
+        csg = sb.tile([P, N], U8, name="csg", align_bytes=256)
+        kwg = sb.tile([P, N], U32, name="kwg", align_bytes=256)
+        k_codes = sb.tile([P, PASSES, N], U16, name="k_codes", align_bytes=256)
         cw0 = load_words(c_words[0], "cw0")
         nc.vector.tensor_copy(ksg[:], ks[:].bitcast(U8).indirect(offsets[:]))
         place(k_plane, 0, ksg)
@@ -100,12 +100,12 @@ def tile_attend_neu_mix_topk_kernel(tc, qT, k_words, k_scales, c_words, c_scales
                 start=(o == 0),
                 stop=(o == PASSES - 1),
             )
-        gate = sb.tile([P, N], F32, name="gate")
+        gate = sb.tile([P, N], F32, name="gate", align_bytes=256)
         nc.scalar.activation(gate[:], a_ps[:], ACT.Sigmoid)
 
         pieces = [slice(c, c + P) for c in range(0, N, P)]
         z_ps = [ps.tile([P, N], F32, name=f"z_ps{h}") for h in range(len(pieces))]
-        cwg = [sb.tile([P, N], U32, name=f"cwg{o}", align_bytes=64) for o in range(PASSES)]
+        cwg = [sb.tile([P, N], U32, name=f"cwg{o}", align_bytes=256) for o in range(PASSES)]
         nc.vector.tensor_copy(cwg[0][:], cw[0][:].bitcast(U32).indirect(offsets[:]))
         for h in range(2):
             slots = slice(h * HALF, (h + 1) * HALF)
@@ -125,7 +125,7 @@ def tile_attend_neu_mix_topk_kernel(tc, qT, k_words, k_scales, c_words, c_scales
                     start=(o == 0),
                     stop=(o == PASSES - 1),
                 )
-        res = sb.tile([P, N], F32, name="res")
+        res = sb.tile([P, N], F32, name="res", align_bytes=256)
         for h, slots in enumerate(pieces):
             nc.vector.tensor_tensor(res[:, slots], z_ps[h][:, slots], gate[:, slots], MULT)
             nc.sync.dma_start(out[0][:, slots], res[:, slots])

@@ -1,4 +1,5 @@
 from contextlib import ExitStack
+from itertools import product
 
 import concourse.mybir as mybir
 
@@ -28,7 +29,7 @@ def tile_attend_neu_mix_topk_kernel(tc, qT, k_words, k_scales, c_words, c_scales
         sb = ctx.enter_context(tc.tile_pool(name="sb", bufs=1))
         ps = ctx.enter_context(tc.psum_pool(name="ps", bufs=1))
 
-        offsets = sb.tile([P, N // 16], U16, name="offsets")
+        offsets = sb.tile([P, N // 16], U16, name="offsets", align_bytes=256)
         q_hbm = qT[0].rearrange("(o p j) w -> p o (j w)", o=PASSES, j=PACK)
         q_raw = [sb.tile([P, PACK * NQ], F32, name=f"q_raw{o}", align_bytes=256) for o in range(PASSES)]
         ks = sb.tile([P, T // 4], I32, name="ks", align_bytes=256)
@@ -113,9 +114,10 @@ def tile_attend_neu_mix_topk_kernel(tc, qT, k_words, k_scales, c_words, c_scales
                 cwg[1][:, slots],
                 cw[1][:].bitcast(U32).indirect(offsets[:, h * HALF // 16 : (h + 1) * HALF // 16]),
             )
-        for h, slots in enumerate(pieces):
-            for o in range(PASSES):
-                cols = slice(o * NQ, (o + 1) * NQ)
+        for first, o in product((0, 2), range(PASSES)):
+            cols = slice(o * NQ, (o + 1) * NQ)
+            for h in (first, first + 1):
+                slots = pieces[h]
                 nc.tensor.matmul_mx(
                     out=z_ps[h][:, slots],
                     lhsT=q_codes[:, cols].bitcast(FP8X4),

@@ -32,7 +32,7 @@ def tile_attend_neu_mix_topk_kernel(tc, qT, k_words, k_scales, c_words, c_scales
         offsets = sb.tile([P, N // 16], U16, name="offsets", align_bytes=256)
         q_hbm = qT[0].rearrange("(o p j) w -> p o (j w)", o=PASSES, j=PACK)
         q_raw = [sb.tile([P, PACK * NQ], F32, name=f"q_raw{o}", align_bytes=256) for o in range(PASSES)]
-        ks = sb.tile([P, T // 4], I32, name="ks", align_bytes=256)
+        ks = sb.tile([P, T // 4], I32, name="ks", tag="ks_then_cw1", align_bytes=256)
         cs = sb.tile([P, T // 4], I32, name="cs", align_bytes=256)
         k_plane = sb.tile([P, PASSES, N // 4], I32, name="k_plane", align_bytes=256)
         c_plane = sb.tile([P, PASSES, N // 4], I32, name="c_plane", align_bytes=256)
@@ -41,14 +41,14 @@ def tile_attend_neu_mix_topk_kernel(tc, qT, k_words, k_scales, c_words, c_scales
         nc.vector.memset(k_plane[:], 0)
         nc.vector.memset(c_plane[:], 0)
 
-        def load_words(words, name):
-            tile = sb.tile([P, T], I32, name=name, align_bytes=256)
+        def load_words(words, name, tag):
+            tile = sb.tile([P, T], I32, name=name, tag=tag, align_bytes=256)
             nc.sync.dma_start(tile[:], words.rearrange("p t b -> p (t b)").bitcast(I32))
             return tile
 
-        def place(plane, first, rows):
+        def place(queue, plane, first, rows):
             for quad in (0, 2, 1, 3):
-                nc.sync.dma_start(
+                queue.dma_start(
                     plane[32 * quad + first : 32 * quad + first + 4, :, :],
                     rows[32 + 16 * quad : 32 + 16 * quad + 16 : 2, :].bitcast(I32),
                 )
@@ -59,7 +59,7 @@ def tile_attend_neu_mix_topk_kernel(tc, qT, k_words, k_scales, c_words, c_scales
         for o in range(PASSES):
             nc.sync.dma_start(ks[32 + 2 * o : 96 : 4, :], k_scales[o].bitcast(I32))
         nc.sync.dma_start(cs[32:96:2, :], c_scales.rearrange("o f t -> f o t").bitcast(I32))
-        kw = load_words(k_words[0], "kw")
+        kw = load_words(k_words[0], "kw", "kw")
 
         q_bf = sb.tile([P, PASSES, NQ, PACK], BF16, name="q_bf", align_bytes=256)
         q_codes = sb.tile([P, PASSES * NQ], U32, name="q_codes", align_bytes=256)
@@ -72,12 +72,12 @@ def tile_attend_neu_mix_topk_kernel(tc, qT, k_words, k_scales, c_words, c_scales
         csg = sb.tile([P, N], U8, name="csg", align_bytes=256)
         kwg = sb.tile([P, N], U32, name="kwg", align_bytes=256)
         k_codes = sb.tile([P, PASSES, N], U16, name="k_codes", align_bytes=256)
-        cw0 = load_words(c_words[0], "cw0")
+        cw0 = load_words(c_words[0], "cw0", "cw0")
         nc.vector.tensor_copy(ksg[:], ks[:].bitcast(U8).indirect(offsets[:]))
-        place(k_plane, 0, ksg)
-        cw = [cw0, load_words(c_words[1], "cw1")]
+        place(nc.scalar, k_plane, 0, ksg)
+        cw = [cw0, load_words(c_words[1], "cw1", "ks_then_cw1")]
         nc.vector.tensor_copy(csg[:], cs[:].bitcast(U8).indirect(offsets[:]))
-        place(c_plane, 4, csg)
+        place(nc.sync, c_plane, 4, csg)
         cast(0)
         cast(1)
         nc.vector.quantize_mx(

@@ -77,7 +77,7 @@ def tile_attend_neu_mix_topk_kernel(tc, qT, k_words, k_scales, c_words, c_scales
         place(nc.scalar, k_plane, 0, ksg)
         cw = [cw0, load_words(c_words[1], "cw1", "ks_then_cw1")]
         nc.vector.tensor_copy(csg[:], cs[:].bitcast(U8).indirect(offsets[:]))
-        place(nc.sync, c_plane, 4, csg)
+        place(nc.scalar, c_plane, 4, csg)
         cast(0)
         cast(1)
         nc.vector.quantize_mx(

@@ -101,6 +101,16 @@ def tile_attend_neu_mix_topk_kernel(tc, qT, k_words, k_scales, c_words, c_scales
                 start=(o == 0),
                 stop=(o == PASSES - 1),
             )
+        warm_ps = ps.tile([P, N], F32, name="warm_ps")
+        nc.tensor.matmul_mx(
+            out=warm_ps[:],
+            lhsT=q_codes[:, NQ:].bitcast(FP8X4),
+            lhsT_scale=q_scales[:, NQ:],
+            rhs=k_codes[:, 1, :].bitcast(FP4X4),
+            rhs_scale=k_plane[:, 1, :].bitcast(U8),
+            start=True,
+            stop=True,
+        )
         gate = sb.tile([P, N], F32, name="gate", align_bytes=256)
         nc.scalar.activation(gate[:], a_ps[:], ACT.Sigmoid)
 

@@ -32,7 +32,7 @@ def tile_attend_neu_mix_topk_kernel(tc, qT, k_words, k_scales, c_words, c_scales
         offsets = sb.tile([P, N // 16], U16, name="offsets", align_bytes=256)
         q_hbm = qT[0].rearrange("(o p j) w -> p o (j w)", o=PASSES, j=PACK)
         q_raw = [sb.tile([P, PACK * NQ], F32, name=f"q_raw{o}", align_bytes=256) for o in range(PASSES)]
-        ks = sb.tile([P, T // 4], I32, name="ks", tag="ks_then_cw1", align_bytes=256)
+        ks = sb.tile([P, T // 4], I32, name="ks", align_bytes=256)
         cs = sb.tile([P, T // 4], I32, name="cs", align_bytes=256)
         k_plane = sb.tile([P, PASSES, N // 4], I32, name="k_plane", align_bytes=256)
         c_plane = sb.tile([P, PASSES, N // 4], I32, name="c_plane", align_bytes=256)
@@ -46,12 +46,19 @@ def tile_attend_neu_mix_topk_kernel(tc, qT, k_words, k_scales, c_words, c_scales
             nc.sync.dma_start(tile[:], words.rearrange("p t b -> p (t b)").bitcast(I32))
             return tile
 
-        def place(queue, plane, first, rows):
+        def place(queue, plane, first, rows, by_pass=()):
             for quad in (0, 2, 1, 3):
-                queue.dma_start(
-                    plane[32 * quad + first : 32 * quad + first + 4, :, :],
-                    rows[32 + 16 * quad : 32 + 16 * quad + 16 : 2, :].bitcast(I32),
-                )
+                if quad in by_pass:
+                    for o in range(PASSES):
+                        queue.dma_start(
+                            plane[32 * quad + first : 32 * quad + first + 4, o, :],
+                            rows[32 + 16 * quad + 2 * o : 32 + 16 * quad + 16 : 4, :].bitcast(I32),
+                        )
+                else:
+                    queue.dma_start(
+                        plane[32 * quad + first : 32 * quad + first + 4, :, :],
+                        rows[32 + 16 * quad : 32 + 16 * quad + 16 : 2, :].bitcast(I32),
+                    )
 
         for o in range(PASSES):
             nc.sync.dma_start(q_raw[o][:], q_hbm[:, o, :])
@@ -74,10 +81,10 @@ def tile_attend_neu_mix_topk_kernel(tc, qT, k_words, k_scales, c_words, c_scales
         k_codes = sb.tile([P, PASSES, N], U16, name="k_codes", align_bytes=256)
         cw0 = load_words(c_words[0], "cw0", "cw0")
         nc.vector.tensor_copy(ksg[:], ks[:].bitcast(U8).indirect(offsets[:]))
-        place(nc.scalar, k_plane, 0, ksg)
-        cw = [cw0, load_words(c_words[1], "cw1", "ks_then_cw1")]
+        place(nc.sync, k_plane, 0, ksg, by_pass=(1, 3))
+        cw = [cw0, load_words(c_words[1], "cw1", "cw1")]
         nc.vector.tensor_copy(csg[:], cs[:].bitcast(U8).indirect(offsets[:]))
-        place(nc.scalar, c_plane, 4, csg)
+        place(nc.sync, c_plane, 4, csg)
         cast(0)
         cast(1)
         nc.vector.quantize_mx(
@@ -101,16 +108,6 @@ def tile_attend_neu_mix_topk_kernel(tc, qT, k_words, k_scales, c_words, c_scales
                 start=(o == 0),
                 stop=(o == PASSES - 1),
             )
-        warm_ps = ps.tile([P, N], F32, name="warm_ps")
-        nc.tensor.matmul_mx(
-            out=warm_ps[:],
-            lhsT=q_codes[:, NQ:].bitcast(FP8X4),
-            lhsT_scale=q_scales[:, NQ:],
-            rhs=k_codes[:, 1, :].bitcast(FP4X4),
-            rhs_scale=k_plane[:, 1, :].bitcast(U8),
-            start=True,
-            stop=True,
-        )
         gate = sb.tile([P, N], F32, name="gate", align_bytes=256)
         nc.scalar.activation(gate[:], a_ps[:], ACT.Sigmoid)
 

@@ -33,7 +33,7 @@ def tile_attend_neu_mix_topk_kernel(tc, qT, k_words, k_scales, c_words, c_scales
         q_hbm = qT[0].rearrange("(o p j) w -> p o (j w)", o=PASSES, j=PACK)
         q_raw = [sb.tile([P, PACK * NQ], F32, name=f"q_raw{o}", align_bytes=256) for o in range(PASSES)]
         ks = sb.tile([P, T // 4], I32, name="ks", align_bytes=256)
-        cs = sb.tile([P, T // 4], I32, name="cs", align_bytes=256)
+        cs = sb.tile([P, T // 4], I32, name="cs", tag="cs_then_cw1", align_bytes=256)
         k_plane = sb.tile([P, PASSES, N // 4], I32, name="k_plane", align_bytes=256)
         c_plane = sb.tile([P, PASSES, N // 4], I32, name="c_plane", align_bytes=256)
         nc.vector.memset(ks[:], 0)
@@ -46,25 +46,22 @@ def tile_attend_neu_mix_topk_kernel(tc, qT, k_words, k_scales, c_words, c_scales
             nc.sync.dma_start(tile[:], words.rearrange("p t b -> p (t b)").bitcast(I32))
             return tile
 
-        def place(queue, plane, first, rows, by_pass=()):
-            for quad in (0, 2, 1, 3):
-                if quad in by_pass:
-                    for o in range(PASSES):
-                        queue.dma_start(
-                            plane[32 * quad + first : 32 * quad + first + 4, o, :],
-                            rows[32 + 16 * quad + 2 * o : 32 + 16 * quad + 16 : 4, :].bitcast(I32),
-                        )
-                else:
-                    queue.dma_start(
-                        plane[32 * quad + first : 32 * quad + first + 4, :, :],
-                        rows[32 + 16 * quad : 32 + 16 * quad + 16 : 2, :].bitcast(I32),
-                    )
+        def place_both(plane, first, rows, quad):
+            nc.sync.dma_start(
+                plane[32 * quad + first : 32 * quad + first + 4, :, :],
+                rows[32 + 16 * quad : 32 + 16 * quad + 16 : 2, :].bitcast(I32),
+            )
+
+        def place_pass(plane, first, rows, quad, o):
+            nc.sync.dma_start(
+                plane[32 * quad + first : 32 * quad + first + 4, o, :],
+                rows[32 + 16 * quad + 2 * o : 32 + 16 * quad + 16 : 4, :].bitcast(I32),
+            )
 
         for o in range(PASSES):
             nc.sync.dma_start(q_raw[o][:], q_hbm[:, o, :])
         nc.sync.dma_start(offsets[:], offs)
-        for o in range(PASSES):
-            nc.sync.dma_start(ks[32 + 2 * o : 96 : 4, :], k_scales[o].bitcast(I32))
+        nc.sync.dma_start(ks[32:96:2, :], k_scales.rearrange("o f t -> f o t").bitcast(I32))
         nc.sync.dma_start(cs[32:96:2, :], c_scales.rearrange("o f t -> f o t").bitcast(I32))
         kw = load_words(k_words[0], "kw", "kw")
 
@@ -81,10 +78,15 @@ def tile_attend_neu_mix_topk_kernel(tc, qT, k_words, k_scales, c_words, c_scales
         k_codes = sb.tile([P, PASSES, N], U16, name="k_codes", align_bytes=256)
         cw0 = load_words(c_words[0], "cw0", "cw0")
         nc.vector.tensor_copy(ksg[:], ks[:].bitcast(U8).indirect(offsets[:]))
-        place(nc.sync, k_plane, 0, ksg, by_pass=(1, 3))
-        cw = [cw0, load_words(c_words[1], "cw1", "cw1")]
+        for quad in (0, 2, 1, 3):
+            place_both(k_plane, 0, ksg, quad)
         nc.vector.tensor_copy(csg[:], cs[:].bitcast(U8).indirect(offsets[:]))
-        place(nc.sync, c_plane, 4, csg)
+        moves = list(product(range(PASSES), (0, 2, 1, 3)))
+        o, quad = moves[0]
+        place_pass(c_plane, 4 + 4 * o, csg, quad, o)
+        cw = [cw0, load_words(c_words[1], "cw1", "cs_then_cw1")]
+        for o, quad in moves[1:]:
+            place_pass(c_plane, 4 + 4 * o, csg, quad, o)
         cast(0)
         cast(1)
         nc.vector.quantize_mx(
@@ -130,7 +132,7 @@ def tile_attend_neu_mix_topk_kernel(tc, qT, k_words, k_scales, c_words, c_scales
                     lhsT=q_codes[:, cols].bitcast(FP8X4),
                     lhsT_scale=q_scales[:, cols],
                     rhs=cwg[o][:, slots].bitcast(FP8X4),
-                    rhs_scale=c_plane[4:P, o, :].bitcast(U8)[:, slots],
+                    rhs_scale=c_plane[4 + 4 * o : P, o, :].bitcast(U8)[:, slots],
                     start=(o == 0),
                     stop=(o == PASSES - 1),
                 )

@@ -52,10 +52,10 @@ def tile_attend_neu_mix_topk_kernel(tc, qT, k_words, k_scales, c_words, c_scales
                 rows[32 + 16 * quad : 32 + 16 * quad + 16 : 2, :].bitcast(I32),
             )
 
-        def place_pass(plane, first, rows, quad, o):
+        def place_pass(plane, first, rows, row, o):
             nc.sync.dma_start(
-                plane[32 * quad + first : 32 * quad + first + 4, o, :],
-                rows[32 + 16 * quad + 2 * o : 32 + 16 * quad + 16 : 4, :].bitcast(I32),
+                plane[first + row : P : 32, o, :],
+                rows[32 + 4 * row + 2 * o : 96 : 16, :].bitcast(I32),
             )
 
         for o in range(PASSES):
@@ -81,7 +81,7 @@ def tile_attend_neu_mix_topk_kernel(tc, qT, k_words, k_scales, c_words, c_scales
         for quad in (0, 2, 1, 3):
             place_both(k_plane, 0, ksg, quad)
         nc.vector.tensor_copy(csg[:], cs[:].bitcast(U8).indirect(offsets[:]))
-        moves = list(product(range(PASSES), (0, 2, 1, 3)))
+        moves = list(product(range(PASSES), range(4)))
         o, quad = moves[0]
         place_pass(c_plane, 4 + 4 * o, csg, quad, o)
         cw = [cw0, load_words(c_words[1], "cw1", "cs_then_cw1")]
@@ -123,9 +123,9 @@ def tile_attend_neu_mix_topk_kernel(tc, qT, k_words, k_scales, c_words, c_scales
                 cwg[1][:, slots],
                 cw[1][:].bitcast(U32).indirect(offsets[:, h * HALF // 16 : (h + 1) * HALF // 16]),
             )
-        for first, o in product((0, 2), range(PASSES)):
+        for o in range(PASSES):
             cols = slice(o * NQ, (o + 1) * NQ)
-            for h in (first, first + 1):
+            for h in range(len(pieces)):
                 slots = pieces[h]
                 nc.tensor.matmul_mx(
                     out=z_ps[h][:, slots],

@@ -35,7 +35,8 @@ def tile_attend_neu_mix_topk_kernel(tc, qT, k_words, k_scales, c_words, c_scales
         ks = sb.tile([P, T // 4], I32, name="ks", align_bytes=256)
         cs = sb.tile([P, T // 4], I32, name="cs", tag="cs_then_cw1", align_bytes=256)
         k_plane = sb.tile([P, PASSES, N // 4], I32, name="k_plane", align_bytes=256)
-        c_plane = sb.tile([P, PASSES, N // 4], I32, name="c_plane", align_bytes=256)
+        c_plane = sb.tile([P, (2 * N - P) // 4], I32, name="c_plane", align_bytes=256)
+        c_cols = [slice(o * (N - P) // 4, (o * (N - P) + N) // 4) for o in range(PASSES)]
         nc.vector.memset(ks[:], 0)
         nc.vector.memset(cs[:], 0)
         nc.vector.memset(k_plane[:], 0)
@@ -54,7 +55,7 @@ def tile_attend_neu_mix_topk_kernel(tc, qT, k_words, k_scales, c_words, c_scales
 
         def place_pass(plane, first, rows, row, o):
             nc.sync.dma_start(
-                plane[first + row : P : 32, o, :],
+                plane[first + row : P : 32, c_cols[o]],
                 rows[32 + 4 * row + 2 * o : 96 : 16, :].bitcast(I32),
             )
 
@@ -98,7 +99,7 @@ def tile_attend_neu_mix_topk_kernel(tc, qT, k_words, k_scales, c_words, c_scales
         pairs = kwg[:].bitcast(U16).rearrange("p (n o) -> p o n", o=PASSES)
         nc.vector.tensor_copy(k_codes[:], pairs)
 
-        a_ps = ps.tile([P, N], F32, name="a_ps")
+        a_ps = ps.tile([P, N], F32, name="a_ps", tag="a_then_z")
         for o in range(PASSES):
             cols = slice(o * NQ, (o + 1) * NQ)
             nc.tensor.matmul_mx(
@@ -114,7 +115,8 @@ def tile_attend_neu_mix_topk_kernel(tc, qT, k_words, k_scales, c_words, c_scales
         nc.scalar.activation(gate[:], a_ps[:], ACT.Sigmoid)
 
         pieces = [slice(c, c + P) for c in range(0, N, P)]
-        z_ps = [ps.tile([P, N], F32, name=f"z_ps{h}") for h in range(len(pieces))]
+        z_ps = [ps.tile([P, N], F32, name=f"z_ps{h}") for h in range(len(pieces) - 1)]
+        z_ps.append(ps.tile([P, N], F32, name="z_last", tag="a_then_z"))
         cwg = [sb.tile([P, N], U32, name=f"cwg{o}", align_bytes=256) for o in range(PASSES)]
         nc.vector.tensor_copy(cwg[0][:], cw[0][:].bitcast(U32).indirect(offsets[:]))
         for h in range(2):
@@ -132,7 +134,7 @@ def tile_attend_neu_mix_topk_kernel(tc, qT, k_words, k_scales, c_words, c_scales
                     lhsT=q_codes[:, cols].bitcast(FP8X4),
                     lhsT_scale=q_scales[:, cols],
                     rhs=cwg[o][:, slots].bitcast(FP8X4),
-                    rhs_scale=c_plane[4 + 4 * o : P, o, :].bitcast(U8)[:, slots],
+                    rhs_scale=c_plane[4 + 4 * o : P, c_cols[o]].bitcast(U8)[:, slots],
                     start=(o == 0),
                     stop=(o == PASSES - 1),
                 )

@@ -35,8 +35,8 @@ def tile_attend_neu_mix_topk_kernel(tc, qT, k_words, k_scales, c_words, c_scales
         ks = sb.tile([P, T // 4], I32, name="ks", align_bytes=256)
         cs = sb.tile([P, T // 4], I32, name="cs", tag="cs_then_cw1", align_bytes=256)
         k_plane = sb.tile([P, PASSES, N // 4], I32, name="k_plane", align_bytes=256)
-        c_plane = sb.tile([P, (2 * N - P) // 4], I32, name="c_plane", align_bytes=256)
-        c_cols = [slice(o * (N - P) // 4, (o * (N - P) + N) // 4) for o in range(PASSES)]
+        c_plane = sb.tile([P, (N + HALF) // 4], I32, name="c_plane", align_bytes=256)
+        c_cols = [slice(o * HALF // 4, (o * HALF + N) // 4) for o in range(PASSES)]
         nc.vector.memset(ks[:], 0)
         nc.vector.memset(cs[:], 0)
         nc.vector.memset(k_plane[:], 0)
@@ -99,46 +99,57 @@ def tile_attend_neu_mix_topk_kernel(tc, qT, k_words, k_scales, c_words, c_scales
         pairs = kwg[:].bitcast(U16).rearrange("p (n o) -> p o n", o=PASSES)
         nc.vector.tensor_copy(k_codes[:], pairs)
 
-        a_ps = ps.tile([P, N], F32, name="a_ps", tag="a_then_z")
-        for o in range(PASSES):
-            cols = slice(o * NQ, (o + 1) * NQ)
-            nc.tensor.matmul_mx(
-                out=a_ps[:],
-                lhsT=q_codes[:, cols].bitcast(FP8X4),
-                lhsT_scale=q_scales[:, cols],
-                rhs=k_codes[:, o, :].bitcast(FP4X4),
-                rhs_scale=k_plane[:, o, :].bitcast(U8),
-                start=(o == 0),
-                stop=(o == PASSES - 1),
-            )
         gate = sb.tile([P, N], F32, name="gate", align_bytes=256)
-        nc.scalar.activation(gate[:], a_ps[:], ACT.Sigmoid)
-
-        pieces = [slice(c, c + P) for c in range(0, N, P)]
-        z_ps = [ps.tile([P, N], F32, name=f"z_ps{h}") for h in range(len(pieces) - 1)]
-        z_ps.append(ps.tile([P, N], F32, name="z_last", tag="a_then_z"))
-        cwg = [sb.tile([P, N], U32, name=f"cwg{o}", align_bytes=256) for o in range(PASSES)]
-        nc.vector.tensor_copy(cwg[0][:], cw[0][:].bitcast(U32).indirect(offsets[:]))
         for h in range(2):
             slots = slice(h * HALF, (h + 1) * HALF)
-            nc.vector.tensor_copy(
-                cwg[1][:, slots],
-                cw[1][:].bitcast(U32).indirect(offsets[:, h * HALF // 16 : (h + 1) * HALF // 16]),
-            )
-        for o in range(PASSES):
-            cols = slice(o * NQ, (o + 1) * NQ)
-            for h in range(len(pieces)):
-                slots = pieces[h]
+            a_ps = ps.tile([P, N], F32, name=f"a_ps{h}", tag=f"bank{h}")
+            for o in range(PASSES):
+                cols = slice(o * NQ, (o + 1) * NQ)
                 nc.tensor.matmul_mx(
-                    out=z_ps[h][:, slots],
+                    out=a_ps[:, 0:HALF],
                     lhsT=q_codes[:, cols].bitcast(FP8X4),
                     lhsT_scale=q_scales[:, cols],
-                    rhs=cwg[o][:, slots].bitcast(FP8X4),
-                    rhs_scale=c_plane[4 + 4 * o : P, c_cols[o]].bitcast(U8)[:, slots],
+                    rhs=k_codes[:, o, slots].bitcast(FP4X4),
+                    rhs_scale=k_plane[:, o, :].bitcast(U8)[:, slots],
                     start=(o == 0),
                     stop=(o == PASSES - 1),
                 )
+            nc.scalar.activation(gate[:, slots], a_ps[:, 0:HALF], ACT.Sigmoid)
+
+        pieces = [slice(c, c + P) for c in range(0, N, P)]
+        z_ps = [ps.tile([P, N], F32, name=f"z_ps{h}", tag=f"bank{h}") for h in range(len(pieces))]
         res = sb.tile([P, N], F32, name="res", align_bytes=256)
-        for h, slots in enumerate(pieces):
-            nc.vector.tensor_tensor(res[:, slots], z_ps[h][:, slots], gate[:, slots], MULT)
-            nc.sync.dma_start(out[0][:, slots], res[:, slots])
+        words = {}
+
+        def gather(o, first, count, tag):
+            tile = sb.tile([P, count * P], U32, name=f"cwg{o}_{first}", tag=tag, align_bytes=256)
+            listed = offsets[:, first * P // 16 : (first + count) * P // 16]
+            nc.vector.tensor_copy(tile[:], cw[o][:].bitcast(U32).indirect(listed))
+            for i in range(count):
+                words[o, first + i] = tile[:, i * P : (i + 1) * P]
+
+        def product_pass(o, h):
+            cols = slice(o * NQ, (o + 1) * NQ)
+            nc.tensor.matmul_mx(
+                out=z_ps[h][:, 0:P],
+                lhsT=q_codes[:, cols].bitcast(FP8X4),
+                lhsT_scale=q_scales[:, cols],
+                rhs=words[o, h].bitcast(FP8X4),
+                rhs_scale=c_plane[4 + 4 * o : P, c_cols[o]].bitcast(U8)[:, pieces[h]],
+                start=(o == 0),
+                stop=(o == PASSES - 1),
+            )
+
+        def finish(h):
+            nc.vector.tensor_tensor(res[:, pieces[h]], z_ps[h][:, 0:P], gate[:, pieces[h]], MULT)
+            nc.sync.dma_start(out[0][:, pieces[h]], res[:, pieces[h]])
+
+        gather(0, 0, 4, "g00")
+        gather(1, 0, 2, "g10")
+        gather(1, 2, 1, "g12")
+        gather(1, 3, 1, "g13")
+        for o in range(PASSES):
+            for h in range(len(pieces)):
+                product_pass(o, h)
+        for h in range(len(pieces)):
+            finish(h)

@@ -35,8 +35,8 @@ def tile_attend_neu_mix_topk_kernel(tc, qT, k_words, k_scales, c_words, c_scales
         ks = sb.tile([P, T // 4], I32, name="ks", align_bytes=256)
         cs = sb.tile([P, T // 4], I32, name="cs", tag="cs_then_cw1", align_bytes=256)
         k_plane = sb.tile([P, PASSES, N // 4], I32, name="k_plane", align_bytes=256)
-        c_plane = sb.tile([P, (N + HALF) // 4], I32, name="c_plane", align_bytes=256)
-        c_cols = [slice(o * HALF // 4, (o * HALF + N) // 4) for o in range(PASSES)]
+        c_plane = sb.tile([P, (2 * N - P) // 4], I32, name="c_plane", align_bytes=256)
+        c_cols = [slice(o * (N - P) // 4, (o * (N - P) + N) // 4) for o in range(PASSES)]
         nc.vector.memset(ks[:], 0)
         nc.vector.memset(cs[:], 0)
         nc.vector.memset(k_plane[:], 0)
@@ -142,7 +142,8 @@ def tile_attend_neu_mix_topk_kernel(tc, qT, k_words, k_scales, c_words, c_scales
 
         def finish(h):
             nc.vector.tensor_tensor(res[:, pieces[h]], z_ps[h][:, 0:P], gate[:, pieces[h]], MULT)
-            nc.sync.dma_start(out[0][:, pieces[h]], res[:, pieces[h]])
+            queue = nc.sync if h % 2 else nc.scalar
+            queue.dma_start(out[0][:, pieces[h]], res[:, pieces[h]])
 
         gather(0, 0, 4, "g00")
         gather(1, 0, 2, "g10")

@@ -116,6 +116,17 @@ def tile_attend_neu_mix_topk_kernel(tc, qT, k_words, k_scales, c_words, c_scales
                 )
             nc.scalar.activation(gate[:, slots], a_ps[:, 0:HALF], ACT.Sigmoid)
 
+        warm = ps.tile([P, N], F32, name="warm")
+        nc.tensor.matmul_mx(
+            out=warm[:, 0:P],
+            lhsT=q_codes[:, NQ : 2 * NQ].bitcast(FP8X4),
+            lhsT_scale=q_scales[:, NQ : 2 * NQ],
+            rhs=k_codes[:, 1, 0:P].bitcast(FP4X4),
+            rhs_scale=k_plane[:, 1, :].bitcast(U8)[:, 0:P],
+            start=True,
+            stop=True,
+        )
+
         pieces = [slice(c, c + P) for c in range(0, N, P)]
         z_ps = [ps.tile([P, N], F32, name=f"z_ps{h}", tag=f"bank{h}") for h in range(len(pieces))]
         res = sb.tile([P, N], F32, name="res", align_bytes=256)

@@ -116,16 +116,19 @@ def tile_attend_neu_mix_topk_kernel(tc, qT, k_words, k_scales, c_words, c_scales
                 )
             nc.scalar.activation(gate[:, slots], a_ps[:, 0:HALF], ACT.Sigmoid)
 
-        warm = ps.tile([P, N], F32, name="warm")
-        nc.tensor.matmul_mx(
-            out=warm[:, 0:P],
-            lhsT=q_codes[:, NQ : 2 * NQ].bitcast(FP8X4),
-            lhsT_scale=q_scales[:, NQ : 2 * NQ],
-            rhs=k_codes[:, 1, 0:P].bitcast(FP4X4),
-            rhs_scale=k_plane[:, 1, :].bitcast(U8)[:, 0:P],
-            start=True,
-            stop=True,
-        )
+        warm = ps.tile([P, N], F32, name="warm", tag="bank1")
+        first = 0
+        for width in (P, P // 2):
+            nc.tensor.matmul_mx(
+                out=warm[:, first : first + width],
+                lhsT=q_codes[:, 0:NQ].bitcast(FP8X4),
+                lhsT_scale=q_scales[:, 0:NQ],
+                rhs=q_codes[:, NQ : NQ + width].bitcast(FP8X4),
+                rhs_scale=q_scales[:, NQ : NQ + width],
+                start=True,
+                stop=True,
+            )
+            first = first + width
 
         pieces = [slice(c, c + P) for c in range(0, N, P)]
         z_ps = [ps.tile([P, N], F32, name=f"z_ps{h}", tag=f"bank{h}") for h in range(len(pieces))]

@@ -116,22 +116,23 @@ def tile_attend_neu_mix_topk_kernel(tc, qT, k_words, k_scales, c_words, c_scales
                 )
             nc.scalar.activation(gate[:, slots], a_ps[:, 0:HALF], ACT.Sigmoid)
 
-        warm = ps.tile([P, N], F32, name="warm", tag="bank1")
+        warm = ps.tile([P, N], F32, name="warm")
         first = 0
         for width in (P, P // 2):
             nc.tensor.matmul_mx(
                 out=warm[:, first : first + width],
-                lhsT=q_codes[:, 0:NQ].bitcast(FP8X4),
-                lhsT_scale=q_scales[:, 0:NQ],
-                rhs=q_codes[:, NQ : NQ + width].bitcast(FP8X4),
-                rhs_scale=q_scales[:, NQ : NQ + width],
+                lhsT=q_codes[:, NQ : 2 * NQ].bitcast(FP8X4),
+                lhsT_scale=q_scales[:, NQ : 2 * NQ],
+                rhs=k_codes[:, 1, 0:width].bitcast(FP4X4),
+                rhs_scale=k_plane[:, 1, :].bitcast(U8)[:, 0:width],
                 start=True,
                 stop=True,
             )
             first = first + width
 
         pieces = [slice(c, c + P) for c in range(0, N, P)]
-        z_ps = [ps.tile([P, N], F32, name=f"z_ps{h}", tag=f"bank{h}") for h in range(len(pieces))]
+        banks = ("bank0", "bank2", "bank3", "bank1")
+        z_ps = [ps.tile([P, N], F32, name=f"z_ps{h}", tag=tag) for h, tag in enumerate(banks)]
         res = sb.tile([P, N], F32, name="res", align_bytes=256)
         words = {}
 
@@ -163,8 +164,7 @@ def tile_attend_neu_mix_topk_kernel(tc, qT, k_words, k_scales, c_words, c_scales
         gather(1, 0, 2, "g10")
         gather(1, 2, 1, "g12")
         gather(1, 3, 1, "g13")
-        for o in range(PASSES):
-            for h in range(len(pieces)):
-                product_pass(o, h)
+        for o, h in ((0, 0), (0, 1), (0, 2), (1, 0), (1, 1), (0, 3), (1, 2), (1, 3)):
+            product_pass(o, h)
         for h in range(len(pieces)):
             finish(h)

@@ -116,15 +116,15 @@ def tile_attend_neu_mix_topk_kernel(tc, qT, k_words, k_scales, c_words, c_scales
                 )
             nc.scalar.activation(gate[:, slots], a_ps[:, 0:HALF], ACT.Sigmoid)
 
-        warm = ps.tile([P, N], F32, name="warm")
+        warm = ps.tile([P, N], F32, name="warm", tag="bank0")
         first = 0
         for width in (P, P // 2):
             nc.tensor.matmul_mx(
                 out=warm[:, first : first + width],
-                lhsT=q_codes[:, NQ : 2 * NQ].bitcast(FP8X4),
-                lhsT_scale=q_scales[:, NQ : 2 * NQ],
-                rhs=k_codes[:, 1, 0:width].bitcast(FP4X4),
-                rhs_scale=k_plane[:, 1, :].bitcast(U8)[:, 0:width],
+                lhsT=q_codes[:, 0:NQ].bitcast(FP8X4),
+                lhsT_scale=q_scales[:, 0:NQ],
+                rhs=q_codes[:, NQ : NQ + width].bitcast(FP8X4),
+                rhs_scale=q_scales[:, NQ : NQ + width],
                 start=True,
                 stop=True,
             )

@@ -35,8 +35,8 @@ def tile_attend_neu_mix_topk_kernel(tc, qT, k_words, k_scales, c_words, c_scales
         ks = sb.tile([P, T // 4], I32, name="ks", align_bytes=256)
         cs = sb.tile([P, T // 4], I32, name="cs", tag="cs_then_cw1", align_bytes=256)
         k_plane = sb.tile([P, PASSES, N // 4], I32, name="k_plane", align_bytes=256)
-        c_plane = sb.tile([P, (2 * N - P) // 4], I32, name="c_plane", align_bytes=256)
-        c_cols = [slice(o * (N - P) // 4, (o * (N - P) + N) // 4) for o in range(PASSES)]
+        c_plane = sb.tile([P, PASSES * N // 4], I32, name="c_plane", align_bytes=256)
+        c_cols = [slice(o * N // 4, (o + 1) * N // 4) for o in range(PASSES)]
         nc.vector.memset(ks[:], 0)
         nc.vector.memset(cs[:], 0)
         nc.vector.memset(k_plane[:], 0)
@@ -164,7 +164,7 @@ def tile_attend_neu_mix_topk_kernel(tc, qT, k_words, k_scales, c_words, c_scales
         gather(1, 0, 2, "g10")
         gather(1, 2, 1, "g12")
         gather(1, 3, 1, "g13")
-        for o, h in ((0, 0), (0, 1), (0, 2), (1, 0), (1, 1), (0, 3), (1, 2), (1, 3)):
+        for o, h in product(range(PASSES), range(len(pieces))):
             product_pass(o, h)
         for h in range(len(pieces)):
             finish(h)

@@ -116,20 +116,6 @@ def tile_attend_neu_mix_topk_kernel(tc, qT, k_words, k_scales, c_words, c_scales
                 )
             nc.scalar.activation(gate[:, slots], a_ps[:, 0:HALF], ACT.Sigmoid)
 
-        warm = ps.tile([P, N], F32, name="warm", tag="bank0")
-        first = 0
-        for width in (P, P // 2):
-            nc.tensor.matmul_mx(
-                out=warm[:, first : first + width],
-                lhsT=q_codes[:, 0:NQ].bitcast(FP8X4),
-                lhsT_scale=q_scales[:, 0:NQ],
-                rhs=q_codes[:, NQ : NQ + width].bitcast(FP8X4),
-                rhs_scale=q_scales[:, NQ : NQ + width],
-                start=True,
-                stop=True,
-            )
-            first = first + width
-
         pieces = [slice(c, c + P) for c in range(0, N, P)]
         banks = ("bank0", "bank2", "bank3", "bank1")
         z_ps = [ps.tile([P, N], F32, name=f"z_ps{h}", tag=tag) for h, tag in enumerate(banks)]

from contextlib import ExitStack
from itertools import product

import concourse.mybir as mybir

NQ, D, T, N = 128, 1024, 2048, 512
FLOPS = 2 * 2 * NQ * D * N

F32 = mybir.dt.float32
BF16 = mybir.dt.bfloat16
I32 = mybir.dt.int32
U32 = mybir.dt.uint32
U16 = mybir.dt.uint16
U8 = mybir.dt.uint8
FP8X4 = mybir.dt.float8_e4m3fn_x4
FP4X4 = mybir.dt.float4_e2m1fn_x4
ACT = mybir.ActivationFunctionType
MULT = mybir.AluOpType.mult

P = 128
PACK = 4
PASSES = D // (P * PACK)
HALF = N // 2


def tile_attend_neu_mix_topk_kernel(tc, qT, k_words, k_scales, c_words, c_scales, offs, out):
    nc = tc.nc
    with ExitStack() as ctx:
        sb = ctx.enter_context(tc.tile_pool(name="sb", bufs=1))
        ps = ctx.enter_context(tc.psum_pool(name="ps", bufs=1))

        offsets = sb.tile([P, N // 16], U16, name="offsets", align_bytes=256)
        q_hbm = qT[0].rearrange("(o p j) w -> p o (j w)", o=PASSES, j=PACK)
        q_raw = [sb.tile([P, PACK * NQ], F32, name=f"q_raw{o}", align_bytes=256) for o in range(PASSES)]
        ks = sb.tile([P, T // 4], I32, name="ks", align_bytes=256)
        cs = sb.tile([P, T // 4], I32, name="cs", tag="cs_then_cw1", align_bytes=256)
        k_plane = sb.tile([P, PASSES, N // 4], I32, name="k_plane", align_bytes=256)
        c_plane = sb.tile([P, PASSES * N // 4], I32, name="c_plane", align_bytes=256)
        c_cols = [slice(o * N // 4, (o + 1) * N // 4) for o in range(PASSES)]
        nc.vector.memset(ks[:], 0)
        nc.vector.memset(cs[:], 0)
        nc.vector.memset(k_plane[:], 0)
        nc.vector.memset(c_plane[:], 0)

        def load_words(words, name, tag):
            tile = sb.tile([P, T], I32, name=name, tag=tag, align_bytes=256)
            nc.sync.dma_start(tile[:], words.rearrange("p t b -> p (t b)").bitcast(I32))
            return tile

        def place_both(plane, first, rows, quad):
            nc.sync.dma_start(
                plane[32 * quad + first : 32 * quad + first + 4, :, :],
                rows[32 + 16 * quad : 32 + 16 * quad + 16 : 2, :].bitcast(I32),
            )

        def place_pass(plane, first, rows, row, o):
            nc.sync.dma_start(
                plane[first + row : P : 32, c_cols[o]],
                rows[32 + 4 * row + 2 * o : 96 : 16, :].bitcast(I32),
            )

        for o in range(PASSES):
            nc.sync.dma_start(q_raw[o][:], q_hbm[:, o, :])
        nc.sync.dma_start(offsets[:], offs)
        nc.sync.dma_start(ks[32:96:2, :], k_scales.rearrange("o f t -> f o t").bitcast(I32))
        nc.sync.dma_start(cs[32:96:2, :], c_scales.rearrange("o f t -> f o t").bitcast(I32))
        kw = load_words(k_words[0], "kw", "kw")

        q_bf = sb.tile([P, PASSES, NQ, PACK], BF16, name="q_bf", align_bytes=256)
        q_codes = sb.tile([P, PASSES * NQ], U32, name="q_codes", align_bytes=256)
        q_scales = sb.tile([P, PASSES * NQ], U8, name="q_scales", align_bytes=256)

        def cast(o):
            nc.scalar.copy(q_bf[:, o, :, :], q_raw[o][:].rearrange("p (j w) -> p w j", j=PACK))

        ksg = sb.tile([P, N], U8, name="ksg", align_bytes=256)
        csg = sb.tile([P, N], U8, name="csg", align_bytes=256)
        kwg = sb.tile([P, N], U32, name="kwg", align_bytes=256)
        k_codes = sb.tile([P, PASSES, N], U16, name="k_codes", align_bytes=256)
        cw0 = load_words(c_words[0], "cw0", "cw0")
        nc.vector.tensor_copy(ksg[:], ks[:].bitcast(U8).indirect(offsets[:]))
        for quad in (0, 2, 1, 3):
            place_both(k_plane, 0, ksg, quad)
        nc.vector.tensor_copy(csg[:], cs[:].bitcast(U8).indirect(offsets[:]))
        moves = list(product(range(PASSES), range(4)))
        o, quad = moves[0]
        place_pass(c_plane, 4 + 4 * o, csg, quad, o)
        cw = [cw0, load_words(c_words[1], "cw1", "cs_then_cw1")]
        for o, quad in moves[1:]:
            place_pass(c_plane, 4 + 4 * o, csg, quad, o)
        cast(0)
        cast(1)
        nc.vector.quantize_mx(
            out=q_codes[:].bitcast(FP8X4),
            scales=q_scales[:],
            in_=q_bf[:].rearrange("p o w j -> p (o w j)"),
        )
        nc.vector.tensor_copy(kwg[:], kw[:].bitcast(U32).indirect(offsets[:]))
        pairs = kwg[:].bitcast(U16).rearrange("p (n o) -> p o n", o=PASSES)
        nc.vector.tensor_copy(k_codes[:], pairs)

        gate = sb.tile([P, N], F32, name="gate", align_bytes=256)
        for h in range(2):
            slots = slice(h * HALF, (h + 1) * HALF)
            a_ps = ps.tile([P, N], F32, name=f"a_ps{h}", tag=f"bank{h}")
            for o in range(PASSES):
                cols = slice(o * NQ, (o + 1) * NQ)
                nc.tensor.matmul_mx(
                    out=a_ps[:, 0:HALF],
                    lhsT=q_codes[:, cols].bitcast(FP8X4),
                    lhsT_scale=q_scales[:, cols],
                    rhs=k_codes[:, o, slots].bitcast(FP4X4),
                    rhs_scale=k_plane[:, o, :].bitcast(U8)[:, slots],
                    start=(o == 0),
                    stop=(o == PASSES - 1),
                )
            nc.scalar.activation(gate[:, slots], a_ps[:, 0:HALF], ACT.Sigmoid)

        pieces = [slice(c, c + P) for c in range(0, N, P)]
        banks = ("bank0", "bank2", "bank3", "bank1")
        z_ps = [ps.tile([P, N], F32, name=f"z_ps{h}", tag=tag) for h, tag in enumerate(banks)]
        res = sb.tile([P, N], F32, name="res", align_bytes=256)
        words = {}

        def gather(o, first, count, tag):
            tile = sb.tile([P, count * P], U32, name=f"cwg{o}_{first}", tag=tag, align_bytes=256)
            listed = offsets[:, first * P // 16 : (first + count) * P // 16]
            nc.vector.tensor_copy(tile[:], cw[o][:].bitcast(U32).indirect(listed))
            for i in range(count):
                words[o, first + i] = tile[:, i * P : (i + 1) * P]

        def product_pass(o, h):
            cols = slice(o * NQ, (o + 1) * NQ)
            nc.tensor.matmul_mx(
                out=z_ps[h][:, 0:P],
                lhsT=q_codes[:, cols].bitcast(FP8X4),
                lhsT_scale=q_scales[:, cols],
                rhs=words[o, h].bitcast(FP8X4),
                rhs_scale=c_plane[4 + 4 * o : P, c_cols[o]].bitcast(U8)[:, pieces[h]],
                start=(o == 0),
                stop=(o == PASSES - 1),
            )

        def finish(h):
            nc.vector.tensor_tensor(res[:, pieces[h]], z_ps[h][:, 0:P], gate[:, pieces[h]], MULT)
            queue = nc.sync if h % 2 else nc.scalar
            queue.dma_start(out[0][:, pieces[h]], res[:, pieces[h]])

        gather(0, 0, 4, "g00")
        gather(1, 0, 2, "g10")
        gather(1, 2, 1, "g12")
        gather(1, 3, 1, "g13")
        for o, h in product(range(PASSES), range(len(pieces))):
            product_pass(o, h)
        for h in range(len(pieces)):
            finish(h)
